import numpy as np, ml_dtypes
CORES = [13,21,141,149]
N = 4
BF = ml_dtypes.bfloat16
def gentries(a):
    return np.ascontiguousarray(a.reshape(8, 16, -1).transpose(0, 2, 1)).reshape(8, -1)
def gtable(e):
    e = np.asarray(e); return np.ascontiguousarray(e.reshape(8, -1, 16).transpose(0, 2, 1)).reshape(128, -1).astype(np.int32)
ND, D, V, Q, TOP = 2048, 10, 96, 512, 1000000
def free(rng):
    s = rng.integers(-TOP, TOP + 1, (8, N * ND, 16))
    c = np.stack([rng.integers(0, (e + 1) * ND, (8, ND, 2)) for e in range(N)], 1).reshape(8, N * ND, 2)
    return s, c
def ledgers(rng):
    s, c = free(rng); G = np.arange(8); roots = []
    ids = np.stack([e * ND + np.argsort(rng.random((8, ND)), 1) for e in range(N)])
    a = rng.integers(-1000, 1001, (8, 1 << D, 16))
    for l in range(D):
        h = 1 << l; n = ids[0][:, h - 1:2 * h - 1]
        s[G[:, None], n] = np.add.reduce(a.reshape(8, h, 2, 1 << (D - 1 - l), 16)[:, :, 0], axis=2)
        if l < D - 1: c[G[:, None], n] = ids[0][:, 2 * h - 1:4 * h - 1].reshape(8, h, 2)
    cur = ids[0][:, 0]
    for e in range(N):
        k = (1 << D) - 1 if e == 0 else 0
        for i in range(V):
            t = rng.integers(0, 1 << D, 8); p = rng.integers(-300, 301, (8, 16)); old = cur; cur = ids[e][:, k]
            for l in range(D):
                b = (t >> (D - 1 - l)) & 1; n = ids[e][:, k]; k += 1
                s[G, n] = s[G, old] + (1 - b)[:, None] * p
                c[G, n] = c[G, old]
                if l < D - 1:
                    old = c[G, old, b]; c[G, n, b] = ids[e][:, k]
            roots.append(cur)
    return s, c, np.stack(roots)
def pack(s, c, ver, day):
    return {"sums": np.ascontiguousarray(s.reshape(8, N, ND, 16).transpose(1, 0, 3, 2)).reshape(N, 128, ND).astype(np.float32),
            "child": np.ascontiguousarray(c.reshape(8, N, 2 * ND).transpose(1, 0, 2)).astype(np.int32),
            "ver": np.stack([gtable(u) for u in ver]), "day": np.stack([gtable(u) for u in day])}
def setup_inputs(rng):
    s, c, roots = ledgers(rng)
    ver = roots[rng.integers(0, N * V, (N, 8, Q)), np.arange(8)[None, :, None]]
    return pack(s, c, ver, rng.integers(0, 1 << D, (N, 8, Q)))
def setup_inputs_any(rng):
    s, c = free(rng)
    return pack(s, c, rng.integers(0, N * ND, (N, 8, Q)), rng.integers(0, 1 << D, (N, 8, Q)))
def setup_inputs_ends(rng):
    s, c = free(rng); e = np.array([0, 1, ND - 2, ND - 1])
    s[:, :, :4] = TOP; s[:, :, 4:8] = -TOP
    c = np.stack([rng.integers(0, q + 1, (8, ND, 2)) * ND + rng.choice(e, (8, ND, 2)) for q in range(N)], 1).reshape(8, N * ND, 2)
    ver = rng.integers(0, N, (N, 8, Q)) * ND + rng.choice(e, (N, 8, Q))
    day = rng.choice(np.array([0, 0, (1 << D) - 1, (1 << D) - 1, (1 << D) - 2] + [1 << l for l in range(D)]), (N, 8, Q))
    ver[:, :, 0] = 0; ver[:, :, Q - 1] = N * ND - 1; day[:, :, 0] = 0; day[:, :, Q - 1] = (1 << D) - 1; day[:, :, 1] = 1; day[:, :, 2] = 1 << (D - 1)
    return pack(s, c, ver, day)
def setup_inputs_crowd(rng):
    s, c = free(rng); q = rng.integers(0, N); p = (q + rng.integers(1, N)) % N
    c[:, q * ND:(q + 1) * ND] = rng.integers(q * ND, (q + 1) * ND, (8, ND, 2))
    ver = rng.integers(q * ND, (q + 1) * ND, (N, 8, Q)); day = rng.integers(0, 1 << D, (N, 8, Q))
    ver[p] = ver[p][:, :1].copy(); day[p] = day[p][:, :1].copy() | 1
    day[p, 0] = (1 << D) - 1; day[p, 7] = (1 << D) - 1
    return pack(s, c, ver, day)
def setup_inputs_older(rng):
    s, c = free(rng)
    for e in range(1, N): c[:, e * ND:(e + 1) * ND] = rng.integers((e - 1) * ND, e * ND, (8, ND, 2))
    c[:, :ND] = np.where(rng.random((8, ND, 2)) < 0.5, np.arange(ND)[None, :, None], c[:, :ND])
    return pack(s, c, rng.integers((N - 1) * ND, N * ND, (N, 8, Q)), rng.integers(0, 1 << D, (N, 8, Q)))
def setup_inputs_spread(rng):
    d = setup_inputs(rng)
    v = rng.integers(-TOP, TOP + 1, (N, 128, ND)) >> (rng.integers(0, 17, (N, 1, ND)) + rng.integers(0, 4, (N, 128, 1)))
    d["sums"] = (v * (rng.random((N, 1, ND)) > 0.0625)).astype(np.float32); return d
def check_inputs(d):
    bad = []; s, c, v, t = d["sums"], d["child"], d["ver"], d["day"]
    if not (np.isfinite(s).all() and (np.abs(s) <= TOP).all() and (s == np.floor(s)).all()): bad.append("sums")
    if not ((c >= 0) & (c < ((np.arange(N) + 1) * ND)[:, None, None])).all(): bad.append("child")
    if not ((v >= 0) & (v < N * ND)).all(): bad.append("ver")
    if not ((t >= 0) & (t < (1 << D))).all(): bad.append("day")
    return bad
def reference(sums, child, ver, day):
    s = np.ascontiguousarray(sums.reshape(N, 8, 16, ND).transpose(1, 0, 3, 2)).reshape(8, N * ND, 16).astype(np.float64)
    c = np.ascontiguousarray(child.transpose(1, 0, 2)).reshape(8, 2 * N * ND).astype(np.int64)
    g = np.arange(8)[:, None]; y = np.zeros((N, 8, Q, 16), np.float64)
    for r in range(N):
        n = gentries(ver[r]).astype(np.int64); t = gentries(day[r]).astype(np.int64)
        for l in range(D - 1, -1, -1):
            b = (t >> l) & 1
            y[r] += b[:, :, None] * s[g, n]
            n = c[g, 2 * n + b]
    return {"y": np.ascontiguousarray(y.transpose(0, 1, 3, 2)).reshape(N, 128, Q).astype(np.float32)}

@@ -1,0 +1,346 @@
+from concourse.bass import DstId, RemoteDMATransfer
+from concourse.mybir import AluOpType, AxisListType, ActivationFunctionType
+
+N, ND, STEPS, Q = 4, 2048, 10, 512
+WORLD = 256
+PW = 256
+SPAD, WPAD = 8, 16
+SW, WW = SPAD + N * ND, WPAD + N * 2 * ND
+H = 65536.0
+FILL = 1024
+NFILL = 8
+
+SCRATCH = {
+    "S": ("sbuf", [128, SW], "float32"),
+    "W": ("sbuf", [128, WW], "float32"),
+    "ct": ("sbuf", [128, 256], "int32"),
+    "cf": ("sbuf", [128, 256], "float32"),
+    "cl": ("dram", [2 * N, 128, 128], "float32"),
+    "hc": ("dram", [128, 128], "float32"),
+    "hin": ("dram", [2, 128, PW], "float32"),
+    "vr": ("sbuf", [128, 32], "int32"),
+    "dn": ("sbuf", [128, 32], "int32"),
+    "ds": ("sbuf", [128, 32], "int32"),
+    "df": ("sbuf", [128, 32], "float32"),
+    "t0": ("sbuf", [128, 32], "float32"),
+    "i0": ("sbuf", [128, 32], "float32"),
+    "bn": ("sbuf", [128, 160], "int32"),
+    "bs": ("sbuf", [128, 160], "int32"),
+    "half": ("sbuf", [128, 160], "float32"),
+    "one": ("sbuf", [128, 128], "float32"),
+    "z0": ("sbuf", [128, 160], "float32"),
+    "z1": ("sbuf", [128, 160], "float32"),
+    "idm": ("sbuf", [128, 128], "float32"),
+    "cols": ("sbuf", [128, 12], "float32"),
+    "dnat": ("sbuf", [128, 640], "float32"),
+    "dswp": ("sbuf", [128, 512], "float32"),
+    "son": ("sbuf", [128, 640], "float32"),
+    "sos": ("sbuf", [128, 640], "float32"),
+    "ow": ("sbuf", [128, 32 * 9], "uint16"),
+    "osm": ("sbuf", [128, 320], "uint16"),
+    "gw": ("sbuf", [128, Q], "float32"),
+    "tw": ("sbuf", [128, Q], "float32"),
+    "gs": ("sbuf", [128, 4 * Q], "float32"),
+    "acc": ("sbuf", [128, Q], "float32"),
+    "yo": ("sbuf", [128, Q], "float32"),
+    "pd": ("psum", [128, 512], "float32"),
+    "pu": ("psum", [128, 512], "float32"),
+    "pa": ("psum", [128, 512], "float32"),
+}
+SEMAPHORES = ["lc", "lq", "ls0", "ls1", "cown", "wd", "st0", "st1", "sent", "parr", "carr", "sarr",
+              "vv", "vhalf", "vw1", "vw2", "vconv", "vday", "vone", "vnat", "vend", "vy0", "vy1",
+              "sw", "sg0", "sg1", "so0", "so1", "sq0", "sq1", "sq2", "sq3", "gz", "gi", "pday", "pun", "pacc"]
+
+A = AluOpType
+NS = 4
+
+
+def mk(engines):
+    return sum(1 << e for e in engines)
+
+
+def plan(T, topo):
+    P = []
+    for r, c in enumerate(T.cores):
+        partner = [q for q, d in enumerate(T.cores) if topo.same_plane(c, d)][0]
+        cross = [q for q in range(N) if q not in (r, partner)]
+        chip = topo.cores_of(c)
+        ports = [k for k in chip if topo.may_write(k, T.cores[cross[0]])]
+        plain = [k for k in chip if k not in ports]
+        near = [k for k in ports if topo.die(k) == topo.die(c)]
+        far = [k for k in ports if k not in near]
+        relays = [k for k in range(WORLD) if topo.mates(k, c) and topo.may_write(k, c)]
+        carriers = [k for k in plain if k != c] + far + near + [c]
+        P.append(dict(core=c, partner=partner, cross=cross, ports=ports, plain=plain, near=near, far=far,
+                      relays=relays, carriers=carriers))
+    return P
+
+
+def relay_of(P, topo, src, k, dst):
+    place = [j for j in P[src]["plain"] if topo.die(j) == topo.die(k)].index(k)
+    return [j for j in P[dst]["relays"] if topo.die(j) == topo.die(k)][place]
+
+
+def window(T, e, p):
+    a = SPAD + e * ND + p * PW
+    return T.S[:, a:a + PW]
+
+
+def did(topo, dst, src):
+    rid, pid = topo.addr(dst, src)
+    return DstId(rid=rid, pnc=pid)
+
+
+def xfer(topo, me, src, dsts, engines, sem):
+    return RemoteDMATransfer(dst_ids=[did(topo, d, me) for d, _ in dsts], dma_engine_mask=mk(engines), remote_sem=sem,
+                             srcs=[src], dsts=[ap for _, ap in dsts])
+
+
+def hop1_engines(P, topo, r):
+    c = P[r]["core"]
+    off = topo.engines(c, P[P[r]["partner"]]["core"])
+    every = topo.engines(c, P[r]["near"][0])
+    on = [e for e in every if e not in off]
+    return [every[t::4] for t in range(4)] + [on[0::2], on[1:4:2], on[5:8:2], off]
+
+
+def helper_program(g, core, T, topo, P):
+    sem = T.sem
+    for r, pr in enumerate(P):
+        if core in pr["carriers"]:
+            p = pr["carriers"].index(core)
+            pc = P[pr["partner"]]["core"]
+            eng = topo.engines(core, pc)
+            n, hf = len(eng), len(eng) // 2
+            sent = 0
+            if core in pr["near"]:
+                par = pr["near"].index(core)
+                g.wait_ge(sem.carr, 4)
+                g.remote_dma_fused([xfer(topo, core, T.hc[:], [(P[q]["core"], T.cl[2 * r + par])], eng[hf * i:hf * (i + 1)], sem.carr)
+                                    for i, q in enumerate(pr["cross"])], local_sem=sem.sent)
+                sent += n
+            g.wait_ge(sem.sarr, len(hop1_engines(P, topo, r)[p]))
+            if core in pr["ports"]:
+                g.remote_dma_fused([xfer(topo, core, T.hin[0], [(P[q]["core"], window(T, r, p)) for q in pr["cross"] + [pr["partner"]]],
+                                         eng, sem.sarr)], local_sem=sem.sent)
+                sent += n
+            else:
+                g.remote_dma_fused([xfer(topo, core, T.hin[0], [(relay_of(P, topo, r, core, q), T.hin[P[q]["cross"].index(r)])],
+                                         eng[hf * i:hf * (i + 1)], sem.sarr) for i, q in enumerate(pr["cross"])], local_sem=sem.sent)
+                g.remote_dma_fused([xfer(topo, core, T.hin[0], [(pc, window(T, r, p))], eng, sem.sarr)], local_sem=sem.sent)
+                sent += 2 * n
+            g.wait_ge(sem.sent, sent)
+        if core in pr["relays"]:
+            eng = topo.engines(core, pr["core"])
+            hf = len(eng) // 2
+            need, moves = 0, []
+            for i, s in enumerate(pr["cross"]):
+                k = [j for j in P[s]["plain"] if relay_of(P, topo, s, j, r) == core][0]
+                n = len(topo.engines(k, core))
+                need += n if k == P[s]["core"] else n // 2
+                moves.append(xfer(topo, core, T.hin[i], [(pr["core"], window(T, s, P[s]["carriers"].index(k)))],
+                                  eng[hf * i:hf * (i + 1)], sem.sarr))
+            g.wait_ge(sem.sarr, need)
+            g.remote_dma_fused(moves, local_sem=sem.sent)
+            g.wait_ge(sem.sent, len(eng))
+
+
+def swap_matmuls(pe, T, out_even, out_odd, even, odd):
+    pe.matmul(out_even, T.z0[:, 16:144], even, True, False)
+    pe.matmul(out_even, T.z0[:, 0:128], odd, False, True)
+    pe.matmul(out_odd, T.z1[:, 16:144], even, True, False)
+    return pe.matmul(out_odd, T.z1[:, 0:128], odd, False, True)
+
+
+def rank_program(g, core, T, topo):
+    P = plan(T, topo)
+    r = T.rank_of(core)
+    if r is None:
+        helper_program(g, core, T, topo, P)
+        return
+    sem, pr = T.sem, P[r]
+    v, s, sy, pe = g.vector, g.scalar, g.sync, g.tensor
+    pc = P[pr["partner"]]["core"]
+    off = topo.engines(core, pc)
+    on = [e for e in topo.engines(core, pr["near"][0]) if e not in off]
+    own = SPAD + r * ND
+    cnt = [0]
+
+    def vop(ins):
+        ins.then_inc(sem.vv, 1)
+        cnt[0] += 1
+
+    def vwait():
+        v.wait_ge(sem.vv, cnt[0])
+
+    def rows(q, par, grp):
+        a = WPAD + q * 2 * ND
+        return T.W[16 * grp + 4 * par:128:32, a:a + 2 * ND], T.cl[2 * q + par]
+
+    sy.dma_start(T.ct[:, 0:128], T.child[0:8:2, :]).then_inc(sem.lc, 16)
+    sy.dma_start(T.ct[:, 128:256], T.child[1:8:2, :]).then_inc(sem.lc, 16)
+    sy.dma_start(T.S[:, own:own + ND // 2], T.sums[:, 0:ND // 2]).then_inc(sem.ls0, 16)
+    sy.dma_start(T.S[:, own + ND // 2:own + ND], T.sums[:, ND // 2:ND]).then_inc(sem.ls1, 16)
+    sy.wait_ge(sem.vconv, 1)
+    for par in range(2):
+        sy.dma_start(T.cl[2 * r + par], T.cf[:, 128 * par:128 * par + 128]).then_inc(sem.cown, 16)
+    sy.wait_ge(sem.cown, 32)
+    sy.wait_ge(sem.vw2, 2)
+    sy.wait_ge(sem.sw, NFILL)
+    for q, wait in ((r, None), (pr["partner"], (sem.parr, len(off))), (pr["cross"][0], (sem.carr, 2 * len(off)))):
+        if wait:
+            sy.wait_ge(*wait)
+        for par in range(2):
+            for grp in range(2):
+                sy.dma_start(*rows(q, par, grp)).then_inc(sem.wd, 16)
+    sy.wait_ge(sem.vy0, 1)
+    sy.dma_start(T.y[:, 0:Q // 2], T.yo[:, 0:Q // 2]).then_inc(sem.st0, 16)
+    sy.wait_ge(sem.st0, 16)
+
+    g.wait_ge(sem.vhalf, 1)
+    for a, z in enumerate((T.z0, T.z1)):
+        g.affine_select(z[:], T.half[:], [[32, 5], [1000, 2], [1, 16]], A.is_equal, 0.0, 16 * a - 1000, -1).then_inc(sem.gz, 1)
+    g.wait_ge(sem.vconv, 1)
+    h4 = len(off) // 2
+    g.remote_dma_fused(
+        [xfer(topo, core, T.cf[:, 128 * par:128 * par + 128], [(pr["near"][par], T.hc[:])], on[h4 * par:h4 * (par + 1)], sem.carr)
+         for par in range(2)] +
+        [xfer(topo, core, T.cf[:, 128 * par:128 * par + 128], [(pc, T.cl[2 * r + par])], off[h4 * par:h4 * (par + 1)], sem.parr)
+         for par in range(2)], local_sem=sem.sent)
+    he = hop1_engines(P, topo, r)
+    g.wait_ge(sem.ls0, 16)
+    g.remote_dma_fused([xfer(topo, core, window(T, r, p), [(pr["carriers"][p], T.hin[0])], he[p], sem.sarr) for p in range(4)],
+                       local_sem=sem.sent)
+    g.wait_ge(sem.ls1, 16)
+    mine = [(relay_of(P, topo, r, core, q), T.hin[P[q]["cross"].index(r)]) for q in pr["cross"]] + [(pc, window(T, r, 7))]
+    g.remote_dma_fused([xfer(topo, core, window(T, r, p), [(pr["carriers"][p], T.hin[0])], he[p], sem.sarr) for p in range(4, 7)] +
+                       [xfer(topo, core, window(T, r, 7), mine, he[7], sem.sarr)], local_sem=sem.sent)
+    g.wait_ge(sem.vone, 1)
+    g.affine_select(T.idm[:], T.one[:], [[-1, 128]], A.is_equal, 0.0, 0, 1).then_inc(sem.gi, 1)
+    g.wait_ge(sem.sent, 2 * (len(off) + len(on)) + sum(len(x) for x in he[0:4]))
+    arrivals = 8 * len(off) + 2 * (4 * len(off) + 4 * h4)
+
+    fill0 = WW - NFILL * FILL
+    v.memset(T.half[:], 0.5).then_inc(sem.vhalf, 1)
+    v.memset(T.W[:, 0:FILL], 0.0).then_inc(sem.vw1, 1)
+    v.memset(T.W[:, FILL:2 * FILL], 0.0).then_inc(sem.vw2, 1)
+    v.wait_ge(sem.lc, 32)
+    v.tensor_scalar(T.cf[:], T.ct[:], 2.0, float(WPAD), A.mult, A.add).then_inc(sem.vconv, 1)
+    v.wait_ge(sem.lq, 32)
+    v.tensor_copy(T.df[:], T.dn[:]).then_inc(sem.vday, 1)
+    v.memset(T.W[:, 2 * FILL:fill0], 0.0).then_inc(sem.vw2, 1)
+    v.memset(T.one[:], 1.0).then_inc(sem.vone, 1)
+    vop(v.memset(T.S[:, 0:SPAD], 0.0))
+    v.wait_ge(sem.pday, 1)
+    vop(v.tensor_scalar(T.ds[:, 0:32:2], T.pd[:, 0:16], 2.0, None, A.mult))
+    vop(v.tensor_scalar(T.ds[:, 1:32:2], T.pd[:, 16:32], 2.0, None, A.mult))
+    v.wait_ge(sem.gz, 2)
+    vop(v.tensor_reduce(T.cols[:, 0:1], T.z0[:], AxisListType.X, A.add))
+    vop(v.tensor_scalar(T.t0[:], T.vr[:], 2.0, float(WPAD), A.mult, A.add))
+    for j in range(5):
+        vop(v.tensor_scalar(T.bn[:, 32 * j:32 * j + 32], T.dn[:], 9 - 2 * j, 1, A.arith_shift_right, A.bitwise_and))
+    vwait()
+    for j in range(5):
+        vop(v.tensor_scalar(T.bs[:, 32 * j:32 * j + 32], T.ds[:], 8 - 2 * j, 1, A.arith_shift_right, A.bitwise_and))
+    vop(v.tensor_tensor(T.i0[:], T.t0[:], T.bn[:, 0:32], A.add))
+    vop(v.tensor_tensor(T.son[:, 3:128:4], T.t0[:], T.bn[:, 0:32], A.mult))
+    vop(v.tensor_scalar(T.cols[:, 4:5], T.cols[:, 0:1], 4 * H, -H, A.mult, A.add))
+    vop(v.tensor_scalar(T.cols[:, 8:9], T.cols[:, 0:1], -2 * H, None, A.mult))
+    vwait()
+    for h, so in enumerate((sem.so0, sem.so1)):
+        v.tensor_copy(T.ow[:, 16 * h:16 * h + 16], T.i0[:, 16 * h:16 * h + 16]).then_inc(so, 1)
+    ev, od = T.bs[:, 0:160:2], T.bs[:, 1:160:2]
+    vop(v.tensor_scalar(T.dnat[:, 0:640:4], T.bs[:], 0.0, -H, A.mult, A.add))
+    vop(v.tensor_scalar(T.dnat[:, 1:640:8], ev, 0.0, H, A.mult, A.add))
+    vop(v.tensor_scalar(T.dnat[:, 5:640:8], od, 0.0, -H, A.mult, A.add))
+    vop(v.tensor_scalar(T.dnat[:, 2:640:8], ev, -H, None, A.add))
+    vop(v.tensor_copy(T.dnat[:, 6:640:8], od))
+    vop(v.tensor_scalar(T.dnat[:, 3:640:4], T.bs[:], H - 1, -H, A.mult, A.add))
+    b4 = T.bn[:, 32:160]
+    vop(v.tensor_scalar(T.dswp[:, 0:512:4], b4, 0.0, -H, A.mult, A.add))
+    vop(v.tensor_scalar(T.dswp[:, 1:512:4], b4, 0.0, T.cols[:, 4:5], A.mult, A.add))
+    vop(v.tensor_scalar(T.dswp[:, 2:512:4], b4, T.cols[:, 8:9], None, A.add))
+    vop(v.tensor_scalar(T.dswp[:, 3:512:4], b4, H - 1, -H, A.mult, A.add))
+    vwait()
+
+    s.dma_start(T.dn[:], T.day[:]).then_inc(sem.lq, 16)
+    s.dma_start(T.vr[:], T.ver[:]).then_inc(sem.lq, 16)
+    s.wait_ge(sem.vw1, 1)
+    for i in range(NFILL):
+        a = fill0 + i * FILL
+        s.activation(T.W[:, a:a + FILL], T.W[:, 0:FILL], ActivationFunctionType.Copy).then_inc(sem.sw, 1)
+    s.wait_ge(sem.sw, NFILL)
+    s.wait_ge(sem.vw2, 2)
+    s.wait_ge(sem.carr, 2 * len(off))
+    for par in range(2):
+        for grp in range(2):
+            s.dma_start(*rows(pr["cross"][1], par, grp)).then_inc(sem.wd, 16)
+    s.wait_ge(sem.wd, 16 * 16)
+
+    pe.wait_ge(sem.gz, 2)
+    pe.wait_ge(sem.vday, 1)
+    swap_matmuls(pe, T, T.pd[:, 0:16], T.pd[:, 16:32], T.df[:, 0:32:2], T.df[:, 1:32:2]).then_inc(sem.pday, 1)
+
+    for k in range(STEPS - 1):
+        j = k // 2
+        for h, (sg, so) in enumerate(((sem.sg0, sem.so0), (sem.sg1, sem.so1))):
+            c0, c1 = 256 * h, 256 * h + 256
+            s.wait_ge(so, k + 1)
+            s.activation(T.gw[:, c0:c1], T.W[:, 0:WW].indirect(T.ow[:, 32 * k + 16 * h:32 * k + 16 * h + 16]),
+                         ActivationFunctionType.Copy).then_inc(sg, 1)
+            v.wait_ge(sg, k + 1)
+            vop(v.transpose(T.tw[:, c0:c1], T.gw[:, c0:c1]))
+            vwait()
+            if k % 2 == 0:
+                d0, res, b = T.dnat, T.sos, 128 * j + 64 * h
+                a = b
+            else:
+                d0, res, b = T.dswp, T.son, 128 * (j + 1) + 64 * h
+                a = b - 128
+            scan = v.tensor_tensor_scan(res[:, b:b + 64], d0[:, a:a + 64], T.tw[:, c0:c1:4], 0.0, A.add, A.max)
+            if k < STEPS - 2:
+                vop(scan)
+                vwait()
+                o = 32 * (k + 1) + 16 * h
+                v.tensor_copy(T.ow[:, o:o + 16], res[:, b + 2:b + 64:4]).then_inc(so, 1)
+            else:
+                scan.then_inc(sem.vend, 1)
+        if k == STEPS - 3:
+            v.tensor_scalar(T.osm[:, 0:160], T.son[:, 3:640:4], 0.5, None, A.mult).then_inc(sem.vnat, 1)
+
+    pe.wait_ge(sem.vend, 2)
+    swap_matmuls(pe, T, T.pu[:, 0:80], T.pu[:, 80:160], T.sos[:, 3:640:8], T.sos[:, 7:640:8]).then_inc(sem.pun, 1)
+    pe.wait_ge(sem.gi, 1)
+    for eng in (s, v):
+        eng.wait_ge(sem.vnat, 1)
+        eng.wait_ge(sem.ls0, 16)
+        eng.wait_ge(sem.ls1, 16)
+        eng.wait_ge(sem.sarr, arrivals)
+
+    def nodes(j):
+        return T.S[:, 0:SW].indirect(T.osm[:, 32 * j:32 * j + 32])
+
+    for j in range(NS):
+        sq = sem["sq%d" % j]
+        s.activation(T.gs[:, Q * j:Q * j + Q], nodes(j), ActivationFunctionType.Copy).then_inc(sq, 1)
+        pe.wait_ge(sq, 1)
+        mm = pe.matmul(T.pa[:], T.idm[:], T.gs[:, Q * j:Q * j + Q], j == 0, j == NS - 1)
+    mm.then_inc(sem.pacc, 1)
+    vop(v.tensor_copy(T.acc[:], nodes(NS)))
+    for j in range(NS + 1, 5):
+        vwait()
+        vop(v.tensor_tensor(T.acc[:], nodes(j), T.acc[:], A.add))
+    v.wait_ge(sem.pun, 1)
+    vop(v.tensor_copy(T.osm[:, 160:320:2], T.pu[:, 0:80]))
+    vop(v.tensor_copy(T.osm[:, 161:320:2], T.pu[:, 80:160]))
+    for j in range(5, STEPS):
+        vwait()
+        vop(v.tensor_tensor(T.acc[:], nodes(j), T.acc[:], A.add))
+    vwait()
+    v.wait_ge(sem.pacc, 1)
+    for h, vy in enumerate((sem.vy0, sem.vy1)):
+        c0, c1 = 256 * h, 256 * h + 256
+        v.tensor_tensor(T.yo[:, c0:c1], T.acc[:, c0:c1], T.pa[:, c0:c1], A.add).then_inc(vy, 1)
+    s.wait_ge(sem.vy1, 1)
+    s.dma_start(T.y[:, Q // 2:Q], T.yo[:, Q // 2:Q]).then_inc(sem.st1, 16)
+    s.wait_ge(sem.st1, 16)

@@ -3,12 +3,12 @@ from concourse.mybir import AluOpType, AxisListType, ActivationFunctionType
 
 N, ND, STEPS, Q = 4, 2048, 10, 512
 WORLD = 256
-PW = 256
-SPAD, WPAD = 8, 16
-SW, WW = SPAD + N * ND, WPAD + N * 2 * ND
-H = 65536.0
-FILL = 1024
-NFILL = 8
+WIDTH = (296, 288)
+SPAD = 8
+SW, EW, WW = SPAD + N * ND, 2 * ND, N * 2 * ND
+H, H2 = 16384, 32768
+VFILL = (2048, 2048, 2048, 2432)
+NAT = 640
 
 SCRATCH = {
     "S": ("sbuf", [128, SW], "float32"),
@@ -17,42 +17,44 @@ SCRATCH = {
     "cf": ("sbuf", [128, 256], "float32"),
     "cl": ("dram", [2 * N, 128, 128], "float32"),
     "hc": ("dram", [128, 128], "float32"),
-    "hin": ("dram", [2, 128, PW], "float32"),
+    "h0": ("dram", [3, 128, WIDTH[0]], "float32"),
+    "h1": ("dram", [3, 128, WIDTH[1]], "float32"),
     "vr": ("sbuf", [128, 32], "int32"),
     "dn": ("sbuf", [128, 32], "int32"),
-    "ds": ("sbuf", [128, 32], "int32"),
     "df": ("sbuf", [128, 32], "float32"),
+    "dd": ("sbuf", [128, 64], "int32"),
+    "bb": ("sbuf", [128, 320], "int32"),
     "t0": ("sbuf", [128, 32], "float32"),
     "i0": ("sbuf", [128, 32], "float32"),
-    "bn": ("sbuf", [128, 160], "int32"),
-    "bs": ("sbuf", [128, 160], "int32"),
     "half": ("sbuf", [128, 160], "float32"),
     "one": ("sbuf", [128, 128], "float32"),
     "z0": ("sbuf", [128, 160], "float32"),
     "z1": ("sbuf", [128, 160], "float32"),
     "idm": ("sbuf", [128, 128], "float32"),
     "cols": ("sbuf", [128, 12], "float32"),
-    "dnat": ("sbuf", [128, 640], "float32"),
-    "dswp": ("sbuf", [128, 512], "float32"),
+    "dc": ("sbuf", [128, NAT + 512], "float32"),
     "son": ("sbuf", [128, 640], "float32"),
     "sos": ("sbuf", [128, 640], "float32"),
     "ow": ("sbuf", [128, 32 * 9], "uint16"),
     "osm": ("sbuf", [128, 320], "uint16"),
     "gw": ("sbuf", [128, Q], "float32"),
     "tw": ("sbuf", [128, Q], "float32"),
-    "gs": ("sbuf", [128, 4 * Q], "float32"),
+    "gs": ("sbuf", [128, 5 * Q], "float32"),
     "acc": ("sbuf", [128, Q], "float32"),
     "yo": ("sbuf", [128, Q], "float32"),
     "pd": ("psum", [128, 512], "float32"),
     "pu": ("psum", [128, 512], "float32"),
-    "pa": ("psum", [128, 512], "float32"),
+    "pv": ("psum", [128, 512], "float32"),
+    "pa0": ("psum", [128, 512], "float32"),
+    "pa1": ("psum", [128, 512], "float32"),
 }
-SEMAPHORES = ["lc", "lq", "ls0", "ls1", "cown", "wd", "st0", "st1", "sent", "parr", "carr", "sarr",
-              "vv", "vhalf", "vw1", "vw2", "vconv", "vday", "vone", "vnat", "vend", "vy0", "vy1",
-              "sw", "sg0", "sg1", "so0", "so1", "sq0", "sq1", "sq2", "sq3", "gz", "gi", "pday", "pun", "pacc"]
+SEMAPHORES = ["lc", "lq", "ls0", "ls1", "wd", "st0", "st1", "sent", "harr", "parr", "carr0", "carr1", "sarr", "ra0", "ra1", "ra2",
+              "vv", "vhalf", "vw1", "vw2", "mz0", "mz1", "mz2", "mz3", "vconv", "vday", "vone", "vnat", "vodd", "vend", "vy0", "vy1",
+              "va0", "va1", "sg0", "sg1", "so0", "so1", "sq0", "sq1", "sq2", "sq3", "sq4", "sq5", "sq6",
+              "gz", "gi", "gk", "pday", "pun", "pen", "pacc0", "pacc1"]
 
 A = AluOpType
-NS = 4
+COPY = ActivationFunctionType.Copy
 
 
 def mk(engines):
@@ -64,26 +66,38 @@ def plan(T, topo):
     for r, c in enumerate(T.cores):
         partner = [q for q, d in enumerate(T.cores) if topo.same_plane(c, d)][0]
         cross = [q for q in range(N) if q not in (r, partner)]
-        chip = topo.cores_of(c)
+        chip = [k for k in topo.cores_of(c) if k != c]
         ports = [k for k in chip if topo.may_write(k, T.cores[cross[0]])]
-        plain = [k for k in chip if k not in ports]
-        near = [k for k in ports if topo.die(k) == topo.die(c)]
-        far = [k for k in ports if k not in near]
+        here = [k for k in chip if topo.die(k) == topo.die(c)]
+        near = [k for k in ports if k in here]
+        far = [k for k in ports if k not in here]
+        plain_near = [k for k in here if k not in ports]
+        plain_far = [k for k in chip if k not in ports and k not in here]
         relays = [k for k in range(WORLD) if topo.mates(k, c) and topo.may_write(k, c)]
-        carriers = [k for k in plain if k != c] + far + near + [c]
-        P.append(dict(core=c, partner=partner, cross=cross, ports=ports, plain=plain, near=near, far=far,
-                      relays=relays, carriers=carriers))
+        carriers = [far[0], near[0], plain_far[0], plain_near[0], far[1], near[1], plain_far[1]]
+        P.append(dict(core=c, partner=partner, cross=cross, ports=ports, near=near, relays=relays, carriers=carriers))
+    for q, pq in enumerate(P):
+        pq["via"] = {}
+        for die in sorted(set(topo.die(k) for k in pq["relays"])):
+            mine = [k for k in pq["relays"] if topo.die(k) == die]
+            items = [(wave(p), s, p) for s in [pq["partner"]] + pq["cross"] for p, k in enumerate(P[s]["carriers"])
+                     if topo.die(k) == die and (k in P[s]["ports"]) == (s == pq["partner"])]
+            for i, (_, s, p) in enumerate(sorted(items)):
+                pq["via"][s, p] = (mine[i % len(mine)], i // len(mine))
     return P
 
 
-def relay_of(P, topo, src, k, dst):
-    place = [j for j in P[src]["plain"] if topo.die(j) == topo.die(k)].index(k)
-    return [j for j in P[dst]["relays"] if topo.die(j) == topo.die(k)][place]
+def wave(p):
+    return p // 4
 
 
 def window(T, e, p):
-    a = SPAD + e * ND + p * PW
-    return T.S[:, a:a + PW]
+    a = SPAD + e * ND + min(p, 4) * WIDTH[0] + max(p - 4, 0) * WIDTH[1]
+    return T.S[:, a:a + WIDTH[wave(p)]]
+
+
+def slot(T, p, i):
+    return (T.h0, T.h1)[wave(p)][i]
 
 
 def did(topo, dst, src):
@@ -96,12 +110,9 @@ def xfer(topo, me, src, dsts, engines, sem):
                              srcs=[src], dsts=[ap for _, ap in dsts])
 
 
-def hop1_engines(P, topo, r):
-    c = P[r]["core"]
-    off = topo.engines(c, P[P[r]["partner"]]["core"])
-    every = topo.engines(c, P[r]["near"][0])
-    on = [e for e in every if e not in off]
-    return [every[t::4] for t in range(4)] + [on[0::2], on[1:4:2], on[5:8:2], off]
+def hand_out_engines(P, topo, r):
+    every = topo.engines(P[r]["core"], P[r]["near"][0])
+    return [every[t::4] for t in range(4)] + [every[0::4], every[1::2], every[2::4]]
 
 
 def helper_program(g, core, T, topo, P):
@@ -109,40 +120,31 @@ def helper_program(g, core, T, topo, P):
     for r, pr in enumerate(P):
         if core in pr["carriers"]:
             p = pr["carriers"].index(core)
-            pc = P[pr["partner"]]["core"]
-            eng = topo.engines(core, pc)
+            eng = topo.engines(core, P[pr["partner"]]["core"])
             n, hf = len(eng), len(eng) // 2
-            sent = 0
+            halves = (eng[:hf], eng[hf:])
+            sent = 2 * n
             if core in pr["near"]:
                 par = pr["near"].index(core)
-                g.wait_ge(sem.carr, 4)
-                g.remote_dma_fused([xfer(topo, core, T.hc[:], [(P[q]["core"], T.cl[2 * r + par])], eng[hf * i:hf * (i + 1)], sem.carr)
-                                    for i, q in enumerate(pr["cross"])], local_sem=sem.sent)
+                g.wait_ge(sem.harr, hf)
+                g.remote_dma_fused([xfer(topo, core, T.hc[:], [(P[q]["core"], T.cl[2 * r + par])], e, sem["carr%d" % P[q]["cross"].index(r)])
+                                    for e, q in zip(halves, pr["cross"])], local_sem=sem.sent)
                 sent += n
-            g.wait_ge(sem.sarr, len(hop1_engines(P, topo, r)[p]))
-            if core in pr["ports"]:
-                g.remote_dma_fused([xfer(topo, core, T.hin[0], [(P[q]["core"], window(T, r, p)) for q in pr["cross"] + [pr["partner"]]],
-                                         eng, sem.sarr)], local_sem=sem.sent)
-                sent += n
-            else:
-                g.remote_dma_fused([xfer(topo, core, T.hin[0], [(relay_of(P, topo, r, core, q), T.hin[P[q]["cross"].index(r)])],
-                                         eng[hf * i:hf * (i + 1)], sem.sarr) for i, q in enumerate(pr["cross"])], local_sem=sem.sent)
-                g.remote_dma_fused([xfer(topo, core, T.hin[0], [(pc, window(T, r, p))], eng, sem.sarr)], local_sem=sem.sent)
-                sent += 2 * n
+            g.wait_ge(sem.sarr, len(hand_out_engines(P, topo, r)[p]))
+            alone, both = ([(eng, pr["partner"])], list(zip(halves, pr["cross"])))
+            relayed, direct = (alone, both) if core in pr["ports"] else (both, alone)
+            g.remote_dma_fused([xfer(topo, core, slot(T, p, 0), [(P[q]["via"][r, p][0], slot(T, p, P[q]["via"][r, p][1]))], e,
+                                     sem["ra%d" % P[q]["via"][r, p][1]]) for e, q in relayed], local_sem=sem.sent)
+            g.remote_dma_fused([xfer(topo, core, slot(T, p, 0), [(P[q]["core"], window(T, r, p))], e, sem.sarr) for e, q in direct],
+                               local_sem=sem.sent)
             g.wait_ge(sem.sent, sent)
         if core in pr["relays"]:
             eng = topo.engines(core, pr["core"])
-            hf = len(eng) // 2
-            need, moves = 0, []
-            for i, s in enumerate(pr["cross"]):
-                k = [j for j in P[s]["plain"] if relay_of(P, topo, s, j, r) == core][0]
-                n = len(topo.engines(k, core))
-                need += n if k == P[s]["core"] else n // 2
-                moves.append(xfer(topo, core, T.hin[i], [(pr["core"], window(T, s, P[s]["carriers"].index(k)))],
-                                  eng[hf * i:hf * (i + 1)], sem.sarr))
-            g.wait_ge(sem.sarr, need)
-            g.remote_dma_fused(moves, local_sem=sem.sent)
-            g.wait_ge(sem.sent, len(eng))
+            mine = sorted((i, s, p) for (s, p), (k, i) in pr["via"].items() if k == core)
+            for i, s, p in mine:
+                g.wait_ge(sem["ra%d" % i], len(eng) if s == pr["partner"] else len(eng) // 2)
+                g.remote_dma_fused([xfer(topo, core, slot(T, p, i), [(pr["core"], window(T, s, p))], eng, sem.sarr)], local_sem=sem.sent)
+            g.wait_ge(sem.sent, len(eng) * len(mine))
 
 
 def swap_matmuls(pe, T, out_even, out_odd, even, odd):
@@ -163,7 +165,11 @@ def rank_program(g, core, T, topo):
     pc = P[pr["partner"]]["core"]
     off = topo.engines(core, pc)
     on = [e for e in topo.engines(core, pr["near"][0]) if e not in off]
-    own = SPAD + r * ND
+    h4 = len(off) // 2
+    own, cut = SPAD + r * ND, 4 * WIDTH[0]
+    order = [r, pr["partner"]] + pr["cross"]
+    w0 = [e * EW for e in order]
+    mz = [sem["mz%d" % i] for i in range(N)]
     cnt = [0]
 
     def vop(ins):
@@ -173,26 +179,23 @@ def rank_program(g, core, T, topo):
     def vwait():
         v.wait_ge(sem.vv, cnt[0])
 
-    def rows(q, par, grp):
-        a = WPAD + q * 2 * ND
-        return T.W[16 * grp + 4 * par:128:32, a:a + 2 * ND], T.cl[2 * q + par]
+    def child_rows(eng, i):
+        for par in range(2):
+            src = T.cl[2 * order[i] + par] if i else T.cf[:, 128 * par:128 * par + 128]
+            for grp in range(2):
+                eng.dma_start(T.W[16 * grp + 4 * par:128:32, w0[i]:w0[i] + EW], src).then_inc(sem.wd, 16)
+
+    clears = [[(VFILL[0], 512), (VFILL[0] + 512, 512), (VFILL[0] + 1024, EW - VFILL[0] - 1024)]]
+    clears += [[(a, min(1024, EW - a)) for a in range(VFILL[i], EW, 1024)] for i in range(1, N)]
+    cleared = [1 + len(c) for c in clears]
 
     sy.dma_start(T.ct[:, 0:128], T.child[0:8:2, :]).then_inc(sem.lc, 16)
-    sy.dma_start(T.ct[:, 128:256], T.child[1:8:2, :]).then_inc(sem.lc, 16)
-    sy.dma_start(T.S[:, own:own + ND // 2], T.sums[:, 0:ND // 2]).then_inc(sem.ls0, 16)
-    sy.dma_start(T.S[:, own + ND // 2:own + ND], T.sums[:, ND // 2:ND]).then_inc(sem.ls1, 16)
-    sy.wait_ge(sem.vconv, 1)
-    for par in range(2):
-        sy.dma_start(T.cl[2 * r + par], T.cf[:, 128 * par:128 * par + 128]).then_inc(sem.cown, 16)
-    sy.wait_ge(sem.cown, 32)
-    sy.wait_ge(sem.vw2, 2)
-    sy.wait_ge(sem.sw, NFILL)
-    for q, wait in ((r, None), (pr["partner"], (sem.parr, len(off))), (pr["cross"][0], (sem.carr, 2 * len(off)))):
-        if wait:
-            sy.wait_ge(*wait)
-        for par in range(2):
-            for grp in range(2):
-                sy.dma_start(*rows(q, par, grp)).then_inc(sem.wd, 16)
+    sy.dma_start(T.S[:, own:own + cut], T.sums[:, 0:cut]).then_inc(sem.ls0, 16)
+    sy.dma_start(T.S[:, own + cut:own + ND], T.sums[:, cut:ND]).then_inc(sem.ls1, 16)
+    for i, arrived in enumerate(((sem.vconv, 1), (sem.parr, len(off)), (sem.carr0, len(off)))):
+        sy.wait_ge(*arrived)
+        sy.wait_ge(mz[i], cleared[i])
+        child_rows(sy, i)
     sy.wait_ge(sem.vy0, 1)
     sy.dma_start(T.y[:, 0:Q // 2], T.yo[:, 0:Q // 2]).then_inc(sem.st0, 16)
     sy.wait_ge(sem.st0, 16)
@@ -201,103 +204,97 @@ def rank_program(g, core, T, topo):
     for a, z in enumerate((T.z0, T.z1)):
         g.affine_select(z[:], T.half[:], [[32, 5], [1000, 2], [1, 16]], A.is_equal, 0.0, 16 * a - 1000, -1).then_inc(sem.gz, 1)
     g.wait_ge(sem.vconv, 1)
-    h4 = len(off) // 2
     g.remote_dma_fused(
-        [xfer(topo, core, T.cf[:, 128 * par:128 * par + 128], [(pr["near"][par], T.hc[:])], on[h4 * par:h4 * (par + 1)], sem.carr)
+        [xfer(topo, core, T.cf[:, 128 * par:128 * par + 128], [(pr["near"][par], T.hc[:])], on[h4 * par:h4 * (par + 1)], sem.harr)
          for par in range(2)] +
         [xfer(topo, core, T.cf[:, 128 * par:128 * par + 128], [(pc, T.cl[2 * r + par])], off[h4 * par:h4 * (par + 1)], sem.parr)
          for par in range(2)], local_sem=sem.sent)
-    he = hop1_engines(P, topo, r)
-    g.wait_ge(sem.ls0, 16)
-    g.remote_dma_fused([xfer(topo, core, window(T, r, p), [(pr["carriers"][p], T.hin[0])], he[p], sem.sarr) for p in range(4)],
-                       local_sem=sem.sent)
-    g.wait_ge(sem.ls1, 16)
-    mine = [(relay_of(P, topo, r, core, q), T.hin[P[q]["cross"].index(r)]) for q in pr["cross"]] + [(pc, window(T, r, 7))]
-    g.remote_dma_fused([xfer(topo, core, window(T, r, p), [(pr["carriers"][p], T.hin[0])], he[p], sem.sarr) for p in range(4, 7)] +
-                       [xfer(topo, core, window(T, r, 7), mine, he[7], sem.sarr)], local_sem=sem.sent)
+    he = hand_out_engines(P, topo, r)
+    for loaded, pieces in ((sem.ls0, range(4)), (sem.ls1, range(4, 7))):
+        g.wait_ge(loaded, 16)
+        g.remote_dma_fused([xfer(topo, core, window(T, r, p), [(pr["carriers"][p], slot(T, p, 0))], he[p], sem.sarr) for p in pieces],
+                           local_sem=sem.sent)
+    g.iota(T.dc[:, 1:NAT:4], [[0, NAT // 8], [-2 * H, 2]], H, 0, allow_small_or_imprecise_dtypes=True).then_inc(sem.gk, 1)
+    g.iota(T.dc[:, 0:NAT + 512:4], [[0, (NAT + 512) // 4]], -H2, 0, allow_small_or_imprecise_dtypes=True).then_inc(sem.gk, 1)
     g.wait_ge(sem.vone, 1)
     g.affine_select(T.idm[:], T.one[:], [[-1, 128]], A.is_equal, 0.0, 0, 1).then_inc(sem.gi, 1)
-    g.wait_ge(sem.sent, 2 * (len(off) + len(on)) + sum(len(x) for x in he[0:4]))
-    arrivals = 8 * len(off) + 2 * (4 * len(off) + 4 * h4)
+    g.wait_ge(sem.sent, len(off) + len(on) + sum(len(x) for x in he))
+    arrivals = 7 * len(off) + 2 * (4 * h4 + 3 * len(off))
 
-    fill0 = WW - NFILL * FILL
     v.memset(T.half[:], 0.5).then_inc(sem.vhalf, 1)
-    v.memset(T.W[:, 0:FILL], 0.0).then_inc(sem.vw1, 1)
-    v.memset(T.W[:, FILL:2 * FILL], 0.0).then_inc(sem.vw2, 1)
+    v.memset(T.W[:, w0[3]:w0[3] + 512], 0.0).then_inc(sem.vw1, 1)
+    v.memset(T.W[:, w0[3] + 512:w0[3] + 1536], 0.0).then_inc(sem.vw2, 1)
     v.wait_ge(sem.lc, 32)
-    v.tensor_scalar(T.cf[:], T.ct[:], 2.0, float(WPAD), A.mult, A.add).then_inc(sem.vconv, 1)
+    v.tensor_scalar(T.cf[:], T.ct[:], 2.0, None, A.mult).then_inc(sem.vconv, 1)
     v.wait_ge(sem.lq, 32)
     v.tensor_copy(T.df[:], T.dn[:]).then_inc(sem.vday, 1)
-    v.memset(T.W[:, 2 * FILL:fill0], 0.0).then_inc(sem.vw2, 1)
-    v.memset(T.one[:], 1.0).then_inc(sem.vone, 1)
-    vop(v.memset(T.S[:, 0:SPAD], 0.0))
+    for i in range(N):
+        a = 1536 if i == 3 else 0
+        v.memset(T.W[:, w0[i] + a:w0[i] + VFILL[i]], 0.0).then_inc(mz[i], 1)
+    vop(v.tensor_copy(T.dd[:, 0:64:2], T.dn[:]))
     v.wait_ge(sem.pday, 1)
-    vop(v.tensor_scalar(T.ds[:, 0:32:2], T.pd[:, 0:16], 2.0, None, A.mult))
-    vop(v.tensor_scalar(T.ds[:, 1:32:2], T.pd[:, 16:32], 2.0, None, A.mult))
-    v.wait_ge(sem.gz, 2)
+    vop(v.tensor_scalar(T.dd[:, 1:64:2], T.pd[:, 0:32], 4.0, None, A.mult))
+    vop(v.tensor_scalar(T.t0[:], T.vr[:], 2.0, float(2 * SPAD), A.mult, A.add))
     vop(v.tensor_reduce(T.cols[:, 0:1], T.z0[:], AxisListType.X, A.add))
-    vop(v.tensor_scalar(T.t0[:], T.vr[:], 2.0, float(WPAD), A.mult, A.add))
-    for j in range(5):
-        vop(v.tensor_scalar(T.bn[:, 32 * j:32 * j + 32], T.dn[:], 9 - 2 * j, 1, A.arith_shift_right, A.bitwise_and))
     vwait()
     for j in range(5):
-        vop(v.tensor_scalar(T.bs[:, 32 * j:32 * j + 32], T.ds[:], 8 - 2 * j, 1, A.arith_shift_right, A.bitwise_and))
-    vop(v.tensor_tensor(T.i0[:], T.t0[:], T.bn[:, 0:32], A.add))
-    vop(v.tensor_tensor(T.son[:, 3:128:4], T.t0[:], T.bn[:, 0:32], A.mult))
-    vop(v.tensor_scalar(T.cols[:, 4:5], T.cols[:, 0:1], 4 * H, -H, A.mult, A.add))
-    vop(v.tensor_scalar(T.cols[:, 8:9], T.cols[:, 0:1], -2 * H, None, A.mult))
+        vop(v.tensor_scalar(T.bb[:, 64 * j:64 * j + 64], T.dd[:], 9 - 2 * j, 1, A.arith_shift_right, A.bitwise_and))
+    vop(v.tensor_scalar(T.cols[:, 4:5], T.cols[:, 0:1], 4.0 * H, -1.0 * H, A.mult, A.add))
+    vop(v.tensor_scalar(T.cols[:, 8:9], T.cols[:, 0:1], -2.0 * H, None, A.mult))
+    vwait()
+    vop(v.tensor_tensor(T.i0[:], T.t0[:], T.bb[:, 0:64:2], A.add))
+    mask = (H2 + 2.0 * SPAD - 1, -1.0 * H2, A.mult, A.add)
+    vop(v.tensor_scalar(T.dc[:, 2:NAT:8], T.bb[:, 1:320:4], -1.0 * H, None, A.add))
+    vop(v.tensor_copy(T.dc[:, 6:NAT:8], T.bb[:, 3:320:4]))
+    vop(v.tensor_scalar(T.dc[:, 3:NAT:4], T.bb[:, 1:320:2], *mask))
     vwait()
     for h, so in enumerate((sem.so0, sem.so1)):
-        v.tensor_copy(T.ow[:, 16 * h:16 * h + 16], T.i0[:, 16 * h:16 * h + 16]).then_inc(so, 1)
-    ev, od = T.bs[:, 0:160:2], T.bs[:, 1:160:2]
-    vop(v.tensor_scalar(T.dnat[:, 0:640:4], T.bs[:], 0.0, -H, A.mult, A.add))
-    vop(v.tensor_scalar(T.dnat[:, 1:640:8], ev, 0.0, H, A.mult, A.add))
-    vop(v.tensor_scalar(T.dnat[:, 5:640:8], od, 0.0, -H, A.mult, A.add))
-    vop(v.tensor_scalar(T.dnat[:, 2:640:8], ev, -H, None, A.add))
-    vop(v.tensor_copy(T.dnat[:, 6:640:8], od))
-    vop(v.tensor_scalar(T.dnat[:, 3:640:4], T.bs[:], H - 1, -H, A.mult, A.add))
-    b4 = T.bn[:, 32:160]
-    vop(v.tensor_scalar(T.dswp[:, 0:512:4], b4, 0.0, -H, A.mult, A.add))
-    vop(v.tensor_scalar(T.dswp[:, 1:512:4], b4, 0.0, T.cols[:, 4:5], A.mult, A.add))
-    vop(v.tensor_scalar(T.dswp[:, 2:512:4], b4, T.cols[:, 8:9], None, A.add))
-    vop(v.tensor_scalar(T.dswp[:, 3:512:4], b4, H - 1, -H, A.mult, A.add))
+        v.tensor_scalar(T.ow[:, 16 * h:16 * h + 16], T.i0[:, 16 * h:16 * h + 16], -2.0 * SPAD, None, A.add).then_inc(so, 1)
+    b4 = T.bb[:, 64:320:2]
+    vop(v.tensor_scalar(T.dc[:, NAT + 1:NAT + 512:4], b4, 0.0, T.cols[:, 4:5], A.mult, A.add))
+    vop(v.tensor_scalar(T.dc[:, NAT + 2:NAT + 512:4], b4, T.cols[:, 8:9], None, A.add))
+    vop(v.tensor_scalar(T.dc[:, NAT + 3:NAT + 512:4], b4, *mask))
+    vop(v.tensor_tensor(T.son[:, 3:128:4], T.t0[:], T.bb[:, 0:64:2], A.mult))
+    vop(v.memset(T.S[:, 0:SPAD], 0.0))
+    v.memset(T.one[:], 1.0).then_inc(sem.vone, 1)
     vwait()
+    v.wait_ge(sem.gk, 2)
 
+    s.dma_start(T.ct[:, 128:256], T.child[1:8:2, :]).then_inc(sem.lc, 16)
     s.dma_start(T.dn[:], T.day[:]).then_inc(sem.lq, 16)
     s.dma_start(T.vr[:], T.ver[:]).then_inc(sem.lq, 16)
     s.wait_ge(sem.vw1, 1)
-    for i in range(NFILL):
-        a = fill0 + i * FILL
-        s.activation(T.W[:, a:a + FILL], T.W[:, 0:FILL], ActivationFunctionType.Copy).then_inc(sem.sw, 1)
-    s.wait_ge(sem.sw, NFILL)
-    s.wait_ge(sem.vw2, 2)
-    s.wait_ge(sem.carr, 2 * len(off))
-    for par in range(2):
-        for grp in range(2):
-            s.dma_start(*rows(pr["cross"][1], par, grp)).then_inc(sem.wd, 16)
+    for i in range(N):
+        for a, n in clears[i]:
+            if (i, a) == (0, VFILL[0] + 1024):
+                s.wait_ge(sem.vw2, 1)
+            s.activation(T.W[:, w0[i] + a:w0[i] + a + n], T.W[:, w0[3]:w0[3] + n], COPY).then_inc(mz[i], 1)
+    for i in range(N):
+        s.wait_ge(mz[i], cleared[i])
+    s.wait_ge(sem.carr1, len(off))
+    child_rows(s, 3)
     s.wait_ge(sem.wd, 16 * 16)
 
     pe.wait_ge(sem.gz, 2)
     pe.wait_ge(sem.vday, 1)
-    swap_matmuls(pe, T, T.pd[:, 0:16], T.pd[:, 16:32], T.df[:, 0:32:2], T.df[:, 1:32:2]).then_inc(sem.pday, 1)
+    swap_matmuls(pe, T, T.pd[:, 0:32:2], T.pd[:, 1:32:2], T.df[:, 0:32:2], T.df[:, 1:32:2]).then_inc(sem.pday, 1)
 
     for k in range(STEPS - 1):
         j = k // 2
         for h, (sg, so) in enumerate(((sem.sg0, sem.so0), (sem.sg1, sem.so1))):
             c0, c1 = 256 * h, 256 * h + 256
             s.wait_ge(so, k + 1)
-            s.activation(T.gw[:, c0:c1], T.W[:, 0:WW].indirect(T.ow[:, 32 * k + 16 * h:32 * k + 16 * h + 16]),
-                         ActivationFunctionType.Copy).then_inc(sg, 1)
+            s.activation(T.gw[:, c0:c1], T.W[:, 0:WW].indirect(T.ow[:, 32 * k + 16 * h:32 * k + 16 * h + 16]), COPY).then_inc(sg, 1)
             v.wait_ge(sg, k + 1)
             vop(v.transpose(T.tw[:, c0:c1], T.gw[:, c0:c1]))
             vwait()
             if k % 2 == 0:
-                d0, res, b = T.dnat, T.sos, 128 * j + 64 * h
+                res, b = T.sos, 128 * j + 64 * h
                 a = b
             else:
-                d0, res, b = T.dswp, T.son, 128 * (j + 1) + 64 * h
-                a = b - 128
-            scan = v.tensor_tensor_scan(res[:, b:b + 64], d0[:, a:a + 64], T.tw[:, c0:c1:4], 0.0, A.add, A.max)
+                res, b = T.son, 128 * (j + 1) + 64 * h
+                a = NAT + b - 128
+            scan = v.tensor_tensor_scan(res[:, b:b + 64], T.dc[:, a:a + 64], T.tw[:, c0:c1:4], 0.0, A.add, A.max)
             if k < STEPS - 2:
                 vop(scan)
                 vwait()
@@ -307,40 +304,51 @@ def rank_program(g, core, T, topo):
                 scan.then_inc(sem.vend, 1)
         if k == STEPS - 3:
             v.tensor_scalar(T.osm[:, 0:160], T.son[:, 3:640:4], 0.5, None, A.mult).then_inc(sem.vnat, 1)
+            v.wait_ge(sem.pun, 1)
+            v.tensor_copy(T.osm[:, 160:288], T.pu[:, 0:128]).then_inc(sem.vodd, 1)
 
+    for so in (sem.so0, sem.so1):
+        pe.wait_ge(so, STEPS - 2)
+    swap_matmuls(pe, T, T.pu[:, 0:128:2], T.pu[:, 1:128:2], T.sos[:, 3:512:8], T.sos[:, 7:512:8]).then_inc(sem.pun, 1)
     pe.wait_ge(sem.vend, 2)
-    swap_matmuls(pe, T, T.pu[:, 0:80], T.pu[:, 80:160], T.sos[:, 3:640:8], T.sos[:, 7:640:8]).then_inc(sem.pun, 1)
-    pe.wait_ge(sem.gi, 1)
+    swap_matmuls(pe, T, T.pv[:, 0:32:2], T.pv[:, 1:32:2], T.sos[:, 515:640:8], T.sos[:, 519:640:8]).then_inc(sem.pen, 1)
+
     for eng in (s, v):
         eng.wait_ge(sem.vnat, 1)
         eng.wait_ge(sem.ls0, 16)
         eng.wait_ge(sem.ls1, 16)
         eng.wait_ge(sem.sarr, arrivals)
+    v.wait_ge(sem.vodd, 1)
 
-    def nodes(j):
-        return T.S[:, 0:SW].indirect(T.osm[:, 32 * j:32 * j + 32])
+    def nodes(j, h=0, n=2):
+        return T.S[:, 0:SW].indirect(T.osm[:, 32 * j + 16 * h:32 * j + 16 * (h + n)])
 
-    for j in range(NS):
-        sq = sem["sq%d" % j]
-        s.activation(T.gs[:, Q * j:Q * j + Q], nodes(j), ActivationFunctionType.Copy).then_inc(sq, 1)
-        pe.wait_ge(sq, 1)
-        mm = pe.matmul(T.pa[:], T.idm[:], T.gs[:, Q * j:Q * j + Q], j == 0, j == NS - 1)
-    mm.then_inc(sem.pacc, 1)
-    vop(v.tensor_copy(T.acc[:], nodes(NS)))
-    for j in range(NS + 1, 5):
-        vwait()
-        vop(v.tensor_tensor(T.acc[:], nodes(j), T.acc[:], A.add))
-    v.wait_ge(sem.pun, 1)
-    vop(v.tensor_copy(T.osm[:, 160:320:2], T.pu[:, 0:80]))
-    vop(v.tensor_copy(T.osm[:, 161:320:2], T.pu[:, 80:160]))
+    pe.wait_ge(sem.gi, 1)
+    pa, va, pacc = (T.pa0, T.pa1), (sem.va0, sem.va1), (sem.pacc0, sem.pacc1)
+    for i, (j, h, n) in enumerate(((0, 0, 1), (0, 1, 1), (1, 0, 1), (1, 1, 1), (2, 0, 2), (3, 0, 2), (4, 0, 2))):
+        sq, a = sem["sq%d" % i], Q * j + 256 * h
+        s.activation(T.gs[:, a:a + 256 * n], nodes(j, h, n), COPY).then_inc(sq, 1)
+        if j:
+            pe.wait_ge(sq, 1)
+            for hh in range(h, h + n):
+                mm = pe.matmul(pa[hh][:, 0:256], T.idm[:], T.gs[:, Q * j + 256 * hh:Q * j + 256 * hh + 256], j == 1, j == 4)
+                if j == 4:
+                    mm.then_inc(pacc[hh], 1)
     for j in range(5, STEPS):
-        vwait()
-        vop(v.tensor_tensor(T.acc[:], nodes(j), T.acc[:], A.add))
-    vwait()
-    v.wait_ge(sem.pacc, 1)
+        if j == STEPS - 2:
+            v.wait_ge(sem.pen, 1)
+            v.tensor_copy(T.osm[:, 288:320], T.pv[:, 0:32]).then_inc(sem.vodd, 1)
+        if j == STEPS - 1:
+            v.wait_ge(sem.vodd, 2)
+        for h in range(2):
+            c0, c1 = 256 * h, 256 * h + 256
+            v.wait_ge(*((va[h], j - 5) if j > 5 else (sem["sq%d" % h], 1)))
+            v.tensor_tensor(T.acc[:, c0:c1], nodes(j, h, 1), (T.acc if j > 5 else T.gs)[:, c0:c1], A.add).then_inc(va[h], 1)
     for h, vy in enumerate((sem.vy0, sem.vy1)):
         c0, c1 = 256 * h, 256 * h + 256
-        v.tensor_tensor(T.yo[:, c0:c1], T.acc[:, c0:c1], T.pa[:, c0:c1], A.add).then_inc(vy, 1)
+        v.wait_ge(va[h], 5)
+        v.wait_ge(pacc[h], 1)
+        v.tensor_tensor(T.yo[:, c0:c1], T.acc[:, c0:c1], pa[h][:, 0:256], A.add).then_inc(vy, 1)
     s.wait_ge(sem.vy1, 1)
     s.dma_start(T.y[:, Q // 2:Q], T.yo[:, Q // 2:Q]).then_inc(sem.st1, 16)
     s.wait_ge(sem.st1, 16)

@@ -1,27 +1,27 @@
 from concourse.bass import DstId, RemoteDMATransfer
-from concourse.mybir import AluOpType, AxisListType, ActivationFunctionType
+from concourse.mybir import AluOpType, ActivationFunctionType
 
 N, ND, STEPS, Q = 4, 2048, 10, 512
 WORLD = 256
-WIDTH = (296, 288)
+WIDTH = (320, 256)
 SPAD = 8
 SW, EW, WW = SPAD + N * ND, 2 * ND, N * 2 * ND
-H, H2 = 16384, 32768
+H = 32768
 VFILL = (2048, 2048, 2048, 2432)
-NAT = 640
+STREAMS = ((0, 10), (10, 20), (20, 32))
+ODD = 640
+OWNQ, PARQ = 256, 384
+BATCHES = ((0, 3, 0, 3), (3, 5, 3, 4), (5, 5, 4, 5))
 
 SCRATCH = {
     "S": ("sbuf", [128, SW], "float32"),
     "W": ("sbuf", [128, WW], "float32"),
-    "ct": ("sbuf", [128, 256], "int32"),
-    "cf": ("sbuf", [128, 256], "float32"),
-    "cl": ("dram", [2 * N, 128, 128], "float32"),
+    "ct": ("sbuf", [128, 320], "int32"),
+    "cf": ("sbuf", [128, 448], "float32"),
+    "cl": ("dram", [N, 128, 128], "float32"),
     "hc": ("dram", [128, 128], "float32"),
     "h0": ("dram", [3, 128, WIDTH[0]], "float32"),
     "h1": ("dram", [3, 128, WIDTH[1]], "float32"),
-    "vr": ("sbuf", [128, 32], "int32"),
-    "dn": ("sbuf", [128, 32], "int32"),
-    "df": ("sbuf", [128, 32], "float32"),
     "dd": ("sbuf", [128, 64], "int32"),
     "bb": ("sbuf", [128, 320], "int32"),
     "t0": ("sbuf", [128, 32], "float32"),
@@ -31,10 +31,11 @@ SCRATCH = {
     "z0": ("sbuf", [128, 160], "float32"),
     "z1": ("sbuf", [128, 160], "float32"),
     "idm": ("sbuf", [128, 128], "float32"),
-    "cols": ("sbuf", [128, 12], "float32"),
-    "dc": ("sbuf", [128, NAT + 512], "float32"),
+    "dc": ("sbuf", [128, ODD + 512], "float32"),
     "son": ("sbuf", [128, 640], "float32"),
     "sos": ("sbuf", [128, 640], "float32"),
+    "tx": ("sbuf", [128, 240], "float32"),
+    "rx": ("sbuf", [128, 240], "float32"),
     "ow": ("sbuf", [128, 32 * 9], "uint16"),
     "osm": ("sbuf", [128, 320], "uint16"),
     "gw": ("sbuf", [128, Q], "float32"),
@@ -42,16 +43,18 @@ SCRATCH = {
     "gs": ("sbuf", [128, 5 * Q], "float32"),
     "acc": ("sbuf", [128, Q], "float32"),
     "yo": ("sbuf", [128, Q], "float32"),
-    "pd": ("psum", [128, 512], "float32"),
-    "pu": ("psum", [128, 512], "float32"),
-    "pv": ("psum", [128, 512], "float32"),
+    "px": ("psum", [128, 512], "float32"),
+    "py": ("psum", [128, 512], "float32"),
+    "pu0": ("psum", [128, 512], "float32"),
+    "pu1": ("psum", [128, 512], "float32"),
+    "pu2": ("psum", [128, 512], "float32"),
     "pa0": ("psum", [128, 512], "float32"),
     "pa1": ("psum", [128, 512], "float32"),
 }
-SEMAPHORES = ["lc", "lq", "ls0", "ls1", "wd", "st0", "st1", "sent", "harr", "parr", "carr0", "carr1", "sarr", "ra0", "ra1", "ra2",
-              "vv", "vhalf", "vw1", "vw2", "mz0", "mz1", "mz2", "mz3", "vconv", "vday", "vone", "vnat", "vodd", "vend", "vy0", "vy1",
-              "va0", "va1", "sg0", "sg1", "so0", "so1", "sq0", "sq1", "sq2", "sq3", "sq4", "sq5", "sq6",
-              "gz", "gi", "gk", "pday", "pun", "pen", "pacc0", "pacc1"]
+SEMAPHORES = ["lc", "ls0", "ls1", "wd", "st0", "st1", "sent", "harr", "parr", "qarr", "carr0", "carr1", "sarr", "ra0", "ra1", "ra2",
+              "lr0", "lr1", "lr2", "vv", "vhalf", "vw1", "vw2", "mz0", "mz1", "mz2", "mz3", "vconv", "vone", "vfirst", "vt", "vs",
+              "vl0", "vl1", "vl2", "vy0", "vy1", "va0", "va1", "sg0", "sg1", "sg2", "so0", "so1", "so2",
+              "sq0", "sq1", "sq2", "sq3", "sq4", "sq5", "sq6", "gz", "gi", "gk", "gt", "pq", "pl0", "pl1", "pl2", "pacc0", "pacc1"]
 
 A = AluOpType
 COPY = ActivationFunctionType.Copy
@@ -75,13 +78,14 @@ def plan(T, topo):
         plain_far = [k for k in chip if k not in ports and k not in here]
         relays = [k for k in range(WORLD) if topo.mates(k, c) and topo.may_write(k, c)]
         carriers = [far[0], near[0], plain_far[0], plain_near[0], far[1], near[1], plain_far[1]]
-        P.append(dict(core=c, partner=partner, cross=cross, ports=ports, near=near, relays=relays, carriers=carriers))
+        P.append(dict(core=c, partner=partner, side=int(r > partner), cross=cross, ports=ports, near=near, relays=relays,
+                      carriers=carriers))
     for q, pq in enumerate(P):
         pq["via"] = {}
         for die in sorted(set(topo.die(k) for k in pq["relays"])):
             mine = [k for k in pq["relays"] if topo.die(k) == die]
-            items = [(wave(p), s, p) for s in [pq["partner"]] + pq["cross"] for p, k in enumerate(P[s]["carriers"])
-                     if topo.die(k) == die and (k in P[s]["ports"]) == (s == pq["partner"])]
+            items = [(wave(p), s, p) for s in pq["cross"] for p, k in enumerate(P[s]["carriers"])
+                     if topo.die(k) == die and relayed(P, s, p, q)]
             for i, (_, s, p) in enumerate(sorted(items)):
                 pq["via"][s, p] = (mine[i % len(mine)], i // len(mine))
     return P
@@ -89,6 +93,11 @@ def plan(T, topo):
 
 def wave(p):
     return p // 4
+
+
+def relayed(P, r, p, q):
+    k = P[r]["carriers"][p]
+    return q != P[r]["partner"] and (k == P[r]["near"][1] or k not in P[r]["ports"])
 
 
 def window(T, e, p):
@@ -105,9 +114,8 @@ def did(topo, dst, src):
     return DstId(rid=rid, pnc=pid)
 
 
-def xfer(topo, me, src, dsts, engines, sem):
-    return RemoteDMATransfer(dst_ids=[did(topo, d, me) for d, _ in dsts], dma_engine_mask=mk(engines), remote_sem=sem,
-                             srcs=[src], dsts=[ap for _, ap in dsts])
+def xfer(topo, me, src, dst, ap, engines, sem):
+    return RemoteDMATransfer(dst_ids=[did(topo, dst, me)], dma_engine_mask=mk(engines), remote_sem=sem, srcs=[src], dsts=[ap])
 
 
 def hand_out_engines(P, topo, r):
@@ -122,36 +130,32 @@ def helper_program(g, core, T, topo, P):
             p = pr["carriers"].index(core)
             eng = topo.engines(core, P[pr["partner"]]["core"])
             n, hf = len(eng), len(eng) // 2
-            halves = (eng[:hf], eng[hf:])
             sent = 2 * n
             if core in pr["near"]:
-                par = pr["near"].index(core)
+                q = [q for q in pr["cross"] if P[q]["side"] == pr["near"].index(core)][0]
                 g.wait_ge(sem.harr, hf)
-                g.remote_dma_fused([xfer(topo, core, T.hc[:], [(P[q]["core"], T.cl[2 * r + par])], e, sem["carr%d" % P[q]["cross"].index(r)])
-                                    for e, q in zip(halves, pr["cross"])], local_sem=sem.sent)
+                g.remote_dma_fused([xfer(topo, core, T.hc[:], P[q]["core"], T.cl[r], eng, sem["carr%d" % P[q]["cross"].index(r)])],
+                                   local_sem=sem.sent)
                 sent += n
             g.wait_ge(sem.sarr, len(hand_out_engines(P, topo, r)[p]))
-            alone, both = ([(eng, pr["partner"])], list(zip(halves, pr["cross"])))
-            relayed, direct = (alone, both) if core in pr["ports"] else (both, alone)
-            g.remote_dma_fused([xfer(topo, core, slot(T, p, 0), [(P[q]["via"][r, p][0], slot(T, p, P[q]["via"][r, p][1]))], e,
-                                     sem["ra%d" % P[q]["via"][r, p][1]]) for e, q in relayed], local_sem=sem.sent)
-            g.remote_dma_fused([xfer(topo, core, slot(T, p, 0), [(P[q]["core"], window(T, r, p))], e, sem.sarr) for e, q in direct],
-                               local_sem=sem.sent)
+            alone, both = ([(eng, pr["partner"])], list(zip((eng[:hf], eng[hf:]), pr["cross"])))
+            for call in ((both, alone) if relayed(P, r, p, pr["cross"][0]) else (alone, both)):
+                moves = []
+                for e, q in call:
+                    if relayed(P, r, p, q):
+                        k, i = P[q]["via"][r, p]
+                        moves.append(xfer(topo, core, slot(T, p, 0), k, slot(T, p, i), e, sem["ra%d" % i]))
+                    else:
+                        moves.append(xfer(topo, core, slot(T, p, 0), P[q]["core"], window(T, r, p), e, sem.sarr))
+                g.remote_dma_fused(moves, local_sem=sem.sent)
             g.wait_ge(sem.sent, sent)
         if core in pr["relays"]:
             eng = topo.engines(core, pr["core"])
             mine = sorted((i, s, p) for (s, p), (k, i) in pr["via"].items() if k == core)
             for i, s, p in mine:
-                g.wait_ge(sem["ra%d" % i], len(eng) if s == pr["partner"] else len(eng) // 2)
-                g.remote_dma_fused([xfer(topo, core, slot(T, p, i), [(pr["core"], window(T, s, p))], eng, sem.sarr)], local_sem=sem.sent)
+                g.wait_ge(sem["ra%d" % i], len(eng) // 2)
+                g.remote_dma_fused([xfer(topo, core, slot(T, p, i), pr["core"], window(T, s, p), eng, sem.sarr)], local_sem=sem.sent)
             g.wait_ge(sem.sent, len(eng) * len(mine))
-
-
-def swap_matmuls(pe, T, out_even, out_odd, even, odd):
-    pe.matmul(out_even, T.z0[:, 16:144], even, True, False)
-    pe.matmul(out_even, T.z0[:, 0:128], odd, False, True)
-    pe.matmul(out_odd, T.z1[:, 16:144], even, True, False)
-    return pe.matmul(out_odd, T.z1[:, 0:128], odd, False, True)
 
 
 def rank_program(g, core, T, topo):
@@ -162,7 +166,7 @@ def rank_program(g, core, T, topo):
         return
     sem, pr = T.sem, P[r]
     v, s, sy, pe = g.vector, g.scalar, g.sync, g.tensor
-    pc = P[pr["partner"]]["core"]
+    pc, side = P[pr["partner"]]["core"], pr["side"]
     off = topo.engines(core, pc)
     on = [e for e in topo.engines(core, pr["near"][0]) if e not in off]
     h4 = len(off) // 2
@@ -179,20 +183,25 @@ def rank_program(g, core, T, topo):
     def vwait():
         v.wait_ge(sem.vv, cnt[0])
 
+    def tile(par):
+        return T.cf[:, 128 * par:128 * par + 128]
+
+    def shift(src, dst):
+        return (T.z0, T.z1)[src][:, 16 - 16 * dst:144 - 16 * dst]
+
     def child_rows(eng, i):
-        for par in range(2):
-            src = T.cl[2 * order[i] + par] if i else T.cf[:, 128 * par:128 * par + 128]
-            for grp in range(2):
-                eng.dma_start(T.W[16 * grp + 4 * par:128:32, w0[i]:w0[i] + EW], src).then_inc(sem.wd, 16)
+        for grp in range(2):
+            eng.dma_start(T.W[16 * grp:128:32, w0[i]:w0[i] + EW], T.cl[order[i]] if i else tile(side)).then_inc(sem.wd, 16)
 
     clears = [[(VFILL[0], 512), (VFILL[0] + 512, 512), (VFILL[0] + 1024, EW - VFILL[0] - 1024)]]
     clears += [[(a, min(1024, EW - a)) for a in range(VFILL[i], EW, 1024)] for i in range(1, N)]
     cleared = [1 + len(c) for c in clears]
 
     sy.dma_start(T.ct[:, 0:128], T.child[0:8:2, :]).then_inc(sem.lc, 16)
+    sy.dma_start(T.ct[:, OWNQ:OWNQ + 32], T.ver[:]).then_inc(sem.lc, 16)
     sy.dma_start(T.S[:, own:own + cut], T.sums[:, 0:cut]).then_inc(sem.ls0, 16)
     sy.dma_start(T.S[:, own + cut:own + ND], T.sums[:, cut:ND]).then_inc(sem.ls1, 16)
-    for i, arrived in enumerate(((sem.vconv, 1), (sem.parr, len(off)), (sem.carr0, len(off)))):
+    for i, arrived in enumerate(((sem.vconv, 1), (sem.parr, h4), (sem.carr0, len(off)))):
         sy.wait_ge(*arrived)
         sy.wait_ge(mz[i], cleared[i])
         child_rows(sy, i)
@@ -205,64 +214,59 @@ def rank_program(g, core, T, topo):
         g.affine_select(z[:], T.half[:], [[32, 5], [1000, 2], [1, 16]], A.is_equal, 0.0, 16 * a - 1000, -1).then_inc(sem.gz, 1)
     g.wait_ge(sem.vconv, 1)
     g.remote_dma_fused(
-        [xfer(topo, core, T.cf[:, 128 * par:128 * par + 128], [(pr["near"][par], T.hc[:])], on[h4 * par:h4 * (par + 1)], sem.harr)
-         for par in range(2)] +
-        [xfer(topo, core, T.cf[:, 128 * par:128 * par + 128], [(pc, T.cl[2 * r + par])], off[h4 * par:h4 * (par + 1)], sem.parr)
-         for par in range(2)], local_sem=sem.sent)
+        [xfer(topo, core, tile(par), pr["near"][par], T.hc[:], on[h4 * par:h4 * (par + 1)], sem.harr) for par in range(2)] +
+        [xfer(topo, core, tile(1 - side), pc, T.cl[r], off[:h4], sem.parr),
+         xfer(topo, core, T.cf[:, OWNQ - 64:OWNQ + 64], pc, T.cf[:, PARQ - 64:PARQ + 64], off[h4:], sem.qarr)], local_sem=sem.sent)
     he = hand_out_engines(P, topo, r)
-    for loaded, pieces in ((sem.ls0, range(4)), (sem.ls1, range(4, 7))):
+
+    def hand_out(loaded, pieces):
         g.wait_ge(loaded, 16)
-        g.remote_dma_fused([xfer(topo, core, window(T, r, p), [(pr["carriers"][p], slot(T, p, 0))], he[p], sem.sarr) for p in pieces],
+        g.remote_dma_fused([xfer(topo, core, window(T, r, p), pr["carriers"][p], slot(T, p, 0), he[p], sem.sarr) for p in pieces],
                            local_sem=sem.sent)
-    g.iota(T.dc[:, 1:NAT:4], [[0, NAT // 8], [-2 * H, 2]], H, 0, allow_small_or_imprecise_dtypes=True).then_inc(sem.gk, 1)
-    g.iota(T.dc[:, 0:NAT + 512:4], [[0, (NAT + 512) // 4]], -H2, 0, allow_small_or_imprecise_dtypes=True).then_inc(sem.gk, 1)
+
+    def start_anew(first):
+        g.iota(T.dc[:, first:ODD + 512:4], [[0, (ODD + 512) // 4]], -H, 0, allow_small_or_imprecise_dtypes=True).then_inc(sem.gk, 1)
+
+    start_anew(0)
+    hand_out(sem.ls0, range(4))
+    hand_out(sem.ls1, range(4, 7))
+    start_anew(3)
     g.wait_ge(sem.vone, 1)
     g.affine_select(T.idm[:], T.one[:], [[-1, 128]], A.is_equal, 0.0, 0, 1).then_inc(sem.gi, 1)
-    g.wait_ge(sem.sent, len(off) + len(on) + sum(len(x) for x in he))
-    arrivals = 7 * len(off) + 2 * (4 * h4 + 3 * len(off))
+    arrivals = sum(len(off) if q == pr["partner"] or relayed(P, q, p, r) else h4 for q in order[1:] for p in range(7))
 
     v.memset(T.half[:], 0.5).then_inc(sem.vhalf, 1)
     v.memset(T.W[:, w0[3]:w0[3] + 512], 0.0).then_inc(sem.vw1, 1)
     v.memset(T.W[:, w0[3] + 512:w0[3] + 1536], 0.0).then_inc(sem.vw2, 1)
-    v.wait_ge(sem.lc, 32)
-    v.tensor_scalar(T.cf[:], T.ct[:], 2.0, None, A.mult).then_inc(sem.vconv, 1)
-    v.wait_ge(sem.lq, 32)
-    v.tensor_copy(T.df[:], T.dn[:]).then_inc(sem.vday, 1)
+    v.wait_ge(sem.lc, 64)
+    v.tensor_scalar(T.cf[:, 0:320], T.ct[:], 2.0, None, A.mult).then_inc(sem.vconv, 1)
+    v.memset(T.one[:], 1.0).then_inc(sem.vone, 1)
     for i in range(N):
         a = 1536 if i == 3 else 0
         v.memset(T.W[:, w0[i] + a:w0[i] + VFILL[i]], 0.0).then_inc(mz[i], 1)
-    vop(v.tensor_copy(T.dd[:, 0:64:2], T.dn[:]))
-    v.wait_ge(sem.pday, 1)
-    vop(v.tensor_scalar(T.dd[:, 1:64:2], T.pd[:, 0:32], 4.0, None, A.mult))
-    vop(v.tensor_scalar(T.t0[:], T.vr[:], 2.0, float(2 * SPAD), A.mult, A.add))
-    vop(v.tensor_reduce(T.cols[:, 0:1], T.z0[:], AxisListType.X, A.add))
+    v.wait_ge(sem.pq, 1)
+    vop(v.tensor_copy(T.dd[:, 0:64:2], T.px[:, 32:64]))
+    vop(v.tensor_scalar(T.dd[:, 1:64:2], T.py[:, 0:32], 2.0, None, A.mult))
+    vop(v.tensor_scalar(T.t0[:], T.px[:, 0:32], 2.0, float(2 * SPAD), A.mult, A.add))
+    vop(v.memset(T.S[:, 0:SPAD], 0.0))
     vwait()
     for j in range(5):
         vop(v.tensor_scalar(T.bb[:, 64 * j:64 * j + 64], T.dd[:], 9 - 2 * j, 1, A.arith_shift_right, A.bitwise_and))
-    vop(v.tensor_scalar(T.cols[:, 4:5], T.cols[:, 0:1], 4.0 * H, -1.0 * H, A.mult, A.add))
-    vop(v.tensor_scalar(T.cols[:, 8:9], T.cols[:, 0:1], -2.0 * H, None, A.mult))
     vwait()
     vop(v.tensor_tensor(T.i0[:], T.t0[:], T.bb[:, 0:64:2], A.add))
-    mask = (H2 + 2.0 * SPAD - 1, -1.0 * H2, A.mult, A.add)
-    vop(v.tensor_scalar(T.dc[:, 2:NAT:8], T.bb[:, 1:320:4], -1.0 * H, None, A.add))
-    vop(v.tensor_copy(T.dc[:, 6:NAT:8], T.bb[:, 3:320:4]))
-    vop(v.tensor_scalar(T.dc[:, 3:NAT:4], T.bb[:, 1:320:2], *mask))
+    mask = (H + 2.0 * SPAD - 1, -1.0 * H, A.mult, A.add)
+    vop(v.tensor_copy(T.dc[:, 1:ODD:4], T.bb[:, 1:320:2]))
+    vop(v.tensor_scalar(T.dc[:, 2:ODD:4], T.bb[:, 1:320:2], *mask))
     vwait()
-    for h, so in enumerate((sem.so0, sem.so1)):
-        v.tensor_scalar(T.ow[:, 16 * h:16 * h + 16], T.i0[:, 16 * h:16 * h + 16], -2.0 * SPAD, None, A.add).then_inc(so, 1)
-    b4 = T.bb[:, 64:320:2]
-    vop(v.tensor_scalar(T.dc[:, NAT + 1:NAT + 512:4], b4, 0.0, T.cols[:, 4:5], A.mult, A.add))
-    vop(v.tensor_scalar(T.dc[:, NAT + 2:NAT + 512:4], b4, T.cols[:, 8:9], None, A.add))
-    vop(v.tensor_scalar(T.dc[:, NAT + 3:NAT + 512:4], b4, *mask))
-    vop(v.tensor_tensor(T.son[:, 3:128:4], T.t0[:], T.bb[:, 0:64:2], A.mult))
-    vop(v.memset(T.S[:, 0:SPAD], 0.0))
-    v.memset(T.one[:], 1.0).then_inc(sem.vone, 1)
+    v.tensor_scalar(T.ow[:, 0:32], T.i0[:], -2.0 * SPAD, None, A.add).then_inc(sem.vfirst, 1)
+    vop(v.tensor_copy(T.dc[:, ODD + 1:ODD + 512:4], T.bb[:, 64:320:2]))
+    vop(v.tensor_scalar(T.dc[:, ODD + 2:ODD + 512:4], T.bb[:, 64:320:2], *mask))
+    vop(v.tensor_tensor(T.son[:, 2:128:4], T.t0[:], T.bb[:, 0:64:2], A.mult))
     vwait()
     v.wait_ge(sem.gk, 2)
 
     s.dma_start(T.ct[:, 128:256], T.child[1:8:2, :]).then_inc(sem.lc, 16)
-    s.dma_start(T.dn[:], T.day[:]).then_inc(sem.lq, 16)
-    s.dma_start(T.vr[:], T.ver[:]).then_inc(sem.lq, 16)
+    s.dma_start(T.ct[:, OWNQ + 32:OWNQ + 64], T.day[:]).then_inc(sem.lc, 16)
     s.wait_ge(sem.vw1, 1)
     for i in range(N):
         for a, n in clears[i]:
@@ -273,77 +277,130 @@ def rank_program(g, core, T, topo):
         s.wait_ge(mz[i], cleared[i])
     s.wait_ge(sem.carr1, len(off))
     child_rows(s, 3)
-    s.wait_ge(sem.wd, 16 * 16)
+    s.wait_ge(sem.wd, 8 * 16)
+
+    def odd_days(q0, par):
+        for c0 in range(2):
+            mm = pe.matmul(T.py[:, par:32:2], shift(side, c0), T.cf[:, q0 + 32 + c0:q0 + 64:2], c0 == 0, c0 == 1)
+        return mm
 
     pe.wait_ge(sem.gz, 2)
-    pe.wait_ge(sem.vday, 1)
-    swap_matmuls(pe, T, T.pd[:, 0:32:2], T.pd[:, 1:32:2], T.df[:, 0:32:2], T.df[:, 1:32:2]).then_inc(sem.pday, 1)
+    pe.wait_ge(sem.vconv, 1)
+    odd_days(OWNQ, side)
+    pe.matmul(T.px[:, 0:64], shift(side, side), T.cf[:, OWNQ:OWNQ + 64], True, False)
+    pe.wait_ge(sem.qarr, h4)
+    pe.matmul(T.px[:, 0:64], shift(side, 1 - side), T.cf[:, PARQ:PARQ + 64], False, True)
+    odd_days(PARQ, 1 - side).then_inc(sem.pq, 1)
 
-    for k in range(STEPS - 1):
-        j = k // 2
-        for h, (sg, so) in enumerate(((sem.sg0, sem.so0), (sem.sg1, sem.so1))):
-            c0, c1 = 256 * h, 256 * h + 256
-            s.wait_ge(so, k + 1)
-            s.activation(T.gw[:, c0:c1], T.W[:, 0:WW].indirect(T.ow[:, 32 * k + 16 * h:32 * k + 16 * h + 16]), COPY).then_inc(sg, 1)
-            v.wait_ge(sg, k + 1)
-            vop(v.transpose(T.tw[:, c0:c1], T.gw[:, c0:c1]))
-            vwait()
-            if k % 2 == 0:
-                res, b = T.sos, 128 * j + 64 * h
-                a = b
-            else:
-                res, b = T.son, 128 * (j + 1) + 64 * h
-                a = NAT + b - 128
-            scan = v.tensor_tensor_scan(res[:, b:b + 64], T.dc[:, a:a + 64], T.tw[:, c0:c1:4], 0.0, A.add, A.max)
-            if k < STEPS - 2:
-                vop(scan)
-                vwait()
-                o = 32 * (k + 1) + 16 * h
-                v.tensor_copy(T.ow[:, o:o + 16], res[:, b + 2:b + 64:4]).then_inc(so, 1)
-            else:
-                scan.then_inc(sem.vend, 1)
-        if k == STEPS - 3:
-            v.tensor_scalar(T.osm[:, 0:160], T.son[:, 3:640:4], 0.5, None, A.mult).then_inc(sem.vnat, 1)
-            v.wait_ge(sem.pun, 1)
-            v.tensor_copy(T.osm[:, 160:288], T.pu[:, 0:128]).then_inc(sem.vodd, 1)
+    def batch(b):
+        a0, a1, c0, c1 = BATCHES[b]
+        x = sum(32 * (u[1] - u[0]) + 16 * (u[3] - u[2]) for u in BATCHES[:b])
+        return a1 - a0, c1 - c0, x, a0 + c0, len(STREAMS) * (a1 + c1 - 1)
 
-    for so in (sem.so0, sem.so1):
-        pe.wait_ge(so, STEPS - 2)
-    swap_matmuls(pe, T, T.pu[:, 0:128:2], T.pu[:, 1:128:2], T.sos[:, 3:512:8], T.sos[:, 7:512:8]).then_inc(sem.pun, 1)
-    pe.wait_ge(sem.vend, 2)
-    swap_matmuls(pe, T, T.pv[:, 0:32:2], T.pv[:, 1:32:2], T.sos[:, 515:640:8], T.sos[:, 519:640:8]).then_inc(sem.pen, 1)
+    def even_nodes(b):
+        return T.son[:, 128 * BATCHES[b][0] + 2:128 * BATCHES[b][1]:4]
+
+    def odd_nodes(b, par):
+        return T.sos[:, 128 * BATCHES[b][2] + 2 + 4 * par:128 * BATCHES[b][3]:8]
+
+    copies = 0
+    for b in range(len(BATCHES)):
+        ne, no, x, _, scans = batch(b)
+        g.wait_ge(sem.vs, scans)
+        for n, a, src in ((32 * ne, x, even_nodes), (16 * no, x + 32 * ne, lambda b: odd_nodes(b, 1 - side))):
+            if n:
+                g.affine_select(T.tx[:, a:a + n], src(b), [[0, n]], A.is_equal, 0.0, 0, 0).then_inc(sem.gt, 1)
+                copies += 1
+        g.wait_ge(sem.gt, copies)
+        width = 32 * ne + 16 * no
+        g.remote_dma_fused([xfer(topo, core, T.tx[:, x:x + width], pc, T.rx[:, x:x + width], off, sem["lr%d" % b])], local_sem=sem.sent)
+    g.wait_ge(sem.sent, (1 + len(BATCHES)) * len(off) + len(on) + sum(len(x) for x in he))
+
+    def turn_lists(b):
+        ne, no, x, _, scans = batch(b)
+        pu = T["pu%d" % b]
+        pe.wait_ge(sem.vs, scans)
+        pe.wait_ge(sem["lr%d" % b], len(off))
+        if ne:
+            pe.matmul(pu[:, 0:32 * ne], shift(side, side), even_nodes(b), True, False)
+            pe.matmul(pu[:, 0:32 * ne], shift(side, 1 - side), T.rx[:, x:x + 32 * ne], False, True)
+        for c0 in range(2):
+            out = pu[:, 32 * ne + c0:32 * (ne + no):2]
+            pe.matmul(out, shift(c0, side), odd_nodes(b, side), True, False)
+            mm = pe.matmul(out, shift(c0, 1 - side), T.rx[:, x + 32 * ne:x + 32 * ne + 16 * no], False, True)
+        mm.then_inc(sem["pl%d" % b], 1)
+
+    def make_offsets(b):
+        ne, no, _, j, _ = batch(b)
+        v.wait_ge(sem["pl%d" % b], 1)
+        v.tensor_copy(T.osm[:, 32 * j:32 * (j + ne + no)], T["pu%d" % b][:, 0:32 * (ne + no)]).then_inc(sem["vl%d" % b], 1)
+
+    slots = [(k, h) for k in range(STEPS - 1) for h in range(len(STREAMS))]
+
+    def scanned(k, h):
+        c0, c1 = STREAMS[h]
+        res, b = (T.son, 128 * (k // 2 + 1)) if k % 2 else (T.sos, 128 * (k // 2))
+        return res, b + 4 * c0, b + 4 * c1
+
+    s.wait_ge(sem.vfirst, 1)
+    for i, (k, h) in enumerate(slots):
+        c0, c1 = STREAMS[h]
+        sg, so = sem["sg%d" % h], sem["so%d" % h]
+        if k:
+            s.wait_ge(so, k)
+        s.activation(T.gw[:, 16 * c0:16 * c1], T.W[:, 0:WW].indirect(T.ow[:, 32 * k + c0:32 * k + c1]), COPY).then_inc(sg, 1)
+        v.wait_ge(sg, k + 1)
+        v.transpose(T.tw[:, 16 * c0:16 * c1], T.gw[:, 16 * c0:16 * c1]).then_inc(sem.vt, 1)
+        if i:
+            v.wait_ge(sem.vs, i)
+            kp, hp = slots[i - 1]
+            if kp < STEPS - 2:
+                res, a, b = scanned(kp, hp)
+                o = 32 * (kp + 1)
+                v.tensor_copy(T.ow[:, o + STREAMS[hp][0]:o + STREAMS[hp][1]], res[:, a + 1:b:4]).then_inc(sem["so%d" % hp], 1)
+        if (k, h) == (STEPS - 2, 1):
+            make_offsets(0)
+        v.wait_ge(sem.vt, i + 1)
+        res, a, b = scanned(k, h)
+        d = 128 * (k // 2) + (ODD if k % 2 else 0)
+        v.tensor_tensor_scan(res[:, a:b], T.dc[:, d + 4 * c0:d + 4 * c1], T.tw[:, 16 * c0:16 * c1:4], 0.0, A.add, A.max).then_inc(sem.vs, 1)
 
     for eng in (s, v):
-        eng.wait_ge(sem.vnat, 1)
+        eng.wait_ge(sem.vl0, 1)
         eng.wait_ge(sem.ls0, 16)
         eng.wait_ge(sem.ls1, 16)
         eng.wait_ge(sem.sarr, arrivals)
-    v.wait_ge(sem.vodd, 1)
 
     def nodes(j, h=0, n=2):
         return T.S[:, 0:SW].indirect(T.osm[:, 32 * j + 16 * h:32 * j + 16 * (h + n)])
 
+    turn_lists(0)
     pe.wait_ge(sem.gi, 1)
     pa, va, pacc = (T.pa0, T.pa1), (sem.va0, sem.va1), (sem.pacc0, sem.pacc1)
-    for i, (j, h, n) in enumerate(((0, 0, 1), (0, 1, 1), (1, 0, 1), (1, 1, 1), (2, 0, 2), (3, 0, 2), (4, 0, 2))):
-        sq, a = sem["sq%d" % i], Q * j + 256 * h
+    for i, (u, j, h, n) in enumerate(((0, 0, 0, 1), (0, 0, 1, 1), (1, 1, 0, 1), (1, 1, 1, 1), (2, 2, 0, 2), (3, 6, 0, 2), (4, 7, 0, 2))):
+        sq, a = sem["sq%d" % i], Q * u + 256 * h
+        if u == 3:
+            s.wait_ge(sem.vl1, 1)
         s.activation(T.gs[:, a:a + 256 * n], nodes(j, h, n), COPY).then_inc(sq, 1)
-        if j:
+        if u:
+            if u in (2, 3):
+                turn_lists(u - 1)
             pe.wait_ge(sq, 1)
             for hh in range(h, h + n):
-                mm = pe.matmul(pa[hh][:, 0:256], T.idm[:], T.gs[:, Q * j + 256 * hh:Q * j + 256 * hh + 256], j == 1, j == 4)
-                if j == 4:
+                mm = pe.matmul(pa[hh][:, 0:256], T.idm[:], T.gs[:, Q * u + 256 * hh:Q * u + 256 * hh + 256], u == 1, u == 4)
+                if u == 4:
                     mm.then_inc(pacc[hh], 1)
-    for j in range(5, STEPS):
-        if j == STEPS - 2:
-            v.wait_ge(sem.pen, 1)
-            v.tensor_copy(T.osm[:, 288:320], T.pv[:, 0:32]).then_inc(sem.vodd, 1)
-        if j == STEPS - 1:
-            v.wait_ge(sem.vodd, 2)
+    for u, j in enumerate((3, 4, 5, 8, 9)):
         for h in range(2):
             c0, c1 = 256 * h, 256 * h + 256
-            v.wait_ge(*((va[h], j - 5) if j > 5 else (sem["sq%d" % h], 1)))
-            v.tensor_tensor(T.acc[:, c0:c1], nodes(j, h, 1), (T.acc if j > 5 else T.gs)[:, c0:c1], A.add).then_inc(va[h], 1)
+            if (j, h) == (5, 1):
+                make_offsets(1)
+            if (j, h) == (8, 1):
+                make_offsets(2)
+            if (j, h) in ((8, 0), (9, 0)):
+                v.wait_ge(sem["vl%d" % (j - 7)], 1)
+            v.wait_ge(*((va[h], u) if u else (sem["sq%d" % h], 1)))
+            v.tensor_tensor(T.acc[:, c0:c1], nodes(j, h, 1), (T.acc if u else T.gs)[:, c0:c1], A.add).then_inc(va[h], 1)
     for h, vy in enumerate((sem.vy0, sem.vy1)):
         c0, c1 = 256 * h, 256 * h + 256
         v.wait_ge(va[h], 5)

@@ -3,31 +3,37 @@ from concourse.mybir import AluOpType, ActivationFunctionType
 
 N, ND, STEPS, Q = 4, 2048, 10, 512
 WORLD = 256
-WIDTH = (320, 256)
+FIRST = 4
+WIDTH = (332, 240)
 SPAD = 8
-SW, EW, WW = SPAD + N * ND, 2 * ND, N * 2 * ND
-H = 32768
-VFILL = (2048, 2048, 2048, 2432)
-STREAMS = ((0, 10), (10, 20), (20, 32))
+SW, WW = SPAD + N * ND, N * ND
+H, H2 = 8192, 32768
+VFILL = (768, 768, 768, 1792)
+STREAMS = ((0, 12), (12, 22), (22, 32))
 ODD = 640
-OWNQ, PARQ = 256, 384
-BATCHES = ((0, 3, 0, 3), (3, 5, 3, 4), (5, 5, 4, 5))
+OWNQ, PARQ = 256, 320
+BATCHES = ((0, 2, 0, 2), (2, 4, 2, 3), (4, 5, 3, 4), (5, 5, 4, 5))
+SHARED = (8, 1)
+ON_SCALAR = [(j, h) for j in (0, 1, 4, 6, 8) for h in range(2)]
+ON_VECTOR = [(j, h) for j in (2, 3, 5) for h in range(2)] + [(7, 1), (7, 0), (8, 1), (9, 0), (9, 1)]
+ADDED = ON_SCALAR[2:7] + [(8, 0), (8, 1), (6, 1)]
+TURN_AT = {(4, 1): 2, (6, 0): 3}
+OFFSETS_AT = {(3, 0): 1, (7, 1): 2, (8, 1): 3}
 
 SCRATCH = {
     "S": ("sbuf", [128, SW], "float32"),
     "W": ("sbuf", [128, WW], "float32"),
-    "ct": ("sbuf", [128, 320], "int32"),
-    "cf": ("sbuf", [128, 448], "float32"),
+    "ct": ("sbuf", [128, 384], "int32"),
+    "cf": ("sbuf", [128, 384], "float32"),
     "cl": ("dram", [N, 128, 128], "float32"),
     "hc": ("dram", [128, 128], "float32"),
     "h0": ("dram", [3, 128, WIDTH[0]], "float32"),
     "h1": ("dram", [3, 128, WIDTH[1]], "float32"),
     "dd": ("sbuf", [128, 64], "int32"),
-    "bb": ("sbuf", [128, 320], "int32"),
+    "be": ("sbuf", [128, 320], "int32"),
+    "bo": ("sbuf", [128, 320], "int32"),
     "t0": ("sbuf", [128, 32], "float32"),
-    "i0": ("sbuf", [128, 32], "float32"),
-    "half": ("sbuf", [128, 160], "float32"),
-    "one": ("sbuf", [128, 128], "float32"),
+    "one": ("sbuf", [128, 160], "float32"),
     "z0": ("sbuf", [128, 160], "float32"),
     "z1": ("sbuf", [128, 160], "float32"),
     "idm": ("sbuf", [128, 128], "float32"),
@@ -48,13 +54,14 @@ SCRATCH = {
     "pu0": ("psum", [128, 512], "float32"),
     "pu1": ("psum", [128, 512], "float32"),
     "pu2": ("psum", [128, 512], "float32"),
+    "pu3": ("psum", [128, 512], "float32"),
     "pa0": ("psum", [128, 512], "float32"),
     "pa1": ("psum", [128, 512], "float32"),
 }
-SEMAPHORES = ["lc", "ls0", "ls1", "wd", "st0", "st1", "sent", "harr", "parr", "qarr", "carr0", "carr1", "sarr", "ra0", "ra1", "ra2",
-              "lr0", "lr1", "lr2", "vv", "vhalf", "vw1", "vw2", "mz0", "mz1", "mz2", "mz3", "vconv", "vone", "vfirst", "vt", "vs",
+SEMAPHORES = ["lc", "lq", "vq", "vqp", "ls0", "ls1", "wd", "st0", "st1", "sent", "harr", "parr", "qarr", "carr0", "carr1", "sarr", "ra0", "ra1", "ra2",
+              "lr0", "lr1", "lr2", "vv", "vw1", "vw2", "mz0", "mz1", "mz2", "mz3", "vconv", "vone", "vfirst", "vt", "vs",
               "vl0", "vl1", "vl2", "vy0", "vy1", "va0", "va1", "sg0", "sg1", "sg2", "so0", "so1", "so2",
-              "sq0", "sq1", "sq2", "sq3", "sq4", "sq5", "sq6", "gz", "gi", "gk", "gt", "pq", "pl0", "pl1", "pl2", "pacc0", "pacc1"]
+              "sq0", "sq1", "sq2", "sq3", "sq4", "sq5", "sq6", "sq7", "sq8", "sq9", "gz", "gi", "gt", "pq", "pl0", "pl1", "pl2", "pl3", "lr3", "vl3", "pacc0", "pacc1"]
 
 A = AluOpType
 COPY = ActivationFunctionType.Copy
@@ -84,15 +91,11 @@ def plan(T, topo):
         pq["via"] = {}
         for die in sorted(set(topo.die(k) for k in pq["relays"])):
             mine = [k for k in pq["relays"] if topo.die(k) == die]
-            items = [(wave(p), s, p) for s in pq["cross"] for p, k in enumerate(P[s]["carriers"])
+            items = [(p, s) for s in range(N) if s != q for p, k in enumerate(P[s]["carriers"])
                      if topo.die(k) == die and relayed(P, s, p, q)]
-            for i, (_, s, p) in enumerate(sorted(items)):
+            for i, (p, s) in enumerate(sorted(items)):
                 pq["via"][s, p] = (mine[i % len(mine)], i // len(mine))
     return P
-
-
-def wave(p):
-    return p // 4
 
 
 def relayed(P, r, p, q):
@@ -100,12 +103,16 @@ def relayed(P, r, p, q):
     return q != P[r]["partner"] and (k == P[r]["near"][1] or k not in P[r]["ports"])
 
 
+def wave(p):
+    return int(p >= FIRST)
+
+
 def window(T, e, p):
-    a = SPAD + e * ND + min(p, 4) * WIDTH[0] + max(p - 4, 0) * WIDTH[1]
+    a = SPAD + e * ND + min(p, FIRST) * WIDTH[0] + max(p - FIRST, 0) * WIDTH[1]
     return T.S[:, a:a + WIDTH[wave(p)]]
 
 
-def slot(T, p, i):
+def slot(T, p, i=0):
     return (T.h0, T.h1)[wave(p)][i]
 
 
@@ -133,7 +140,7 @@ def helper_program(g, core, T, topo, P):
             sent = 2 * n
             if core in pr["near"]:
                 q = [q for q in pr["cross"] if P[q]["side"] == pr["near"].index(core)][0]
-                g.wait_ge(sem.harr, hf)
+                g.wait_ge(sem.harr, n)
                 g.remote_dma_fused([xfer(topo, core, T.hc[:], P[q]["core"], T.cl[r], eng, sem["carr%d" % P[q]["cross"].index(r)])],
                                    local_sem=sem.sent)
                 sent += n
@@ -144,16 +151,16 @@ def helper_program(g, core, T, topo, P):
                 for e, q in call:
                     if relayed(P, r, p, q):
                         k, i = P[q]["via"][r, p]
-                        moves.append(xfer(topo, core, slot(T, p, 0), k, slot(T, p, i), e, sem["ra%d" % i]))
+                        moves.append(xfer(topo, core, slot(T, p), k, slot(T, p, i), e, sem["ra%d" % i]))
                     else:
-                        moves.append(xfer(topo, core, slot(T, p, 0), P[q]["core"], window(T, r, p), e, sem.sarr))
+                        moves.append(xfer(topo, core, slot(T, p), P[q]["core"], window(T, r, p), e, sem.sarr))
                 g.remote_dma_fused(moves, local_sem=sem.sent)
             g.wait_ge(sem.sent, sent)
         if core in pr["relays"]:
             eng = topo.engines(core, pr["core"])
             mine = sorted((i, s, p) for (s, p), (k, i) in pr["via"].items() if k == core)
             for i, s, p in mine:
-                g.wait_ge(sem["ra%d" % i], len(eng) // 2)
+                g.wait_ge(sem["ra%d" % i], len(eng) if s == pr["partner"] else len(eng) // 2)
                 g.remote_dma_fused([xfer(topo, core, slot(T, p, i), pr["core"], window(T, s, p), eng, sem.sarr)], local_sem=sem.sent)
             g.wait_ge(sem.sent, len(eng) * len(mine))
 
@@ -170,9 +177,9 @@ def rank_program(g, core, T, topo):
     off = topo.engines(core, pc)
     on = [e for e in topo.engines(core, pr["near"][0]) if e not in off]
     h4 = len(off) // 2
-    own, cut = SPAD + r * ND, 4 * WIDTH[0]
+    own, cut = SPAD + r * ND, FIRST * WIDTH[0]
     order = [r, pr["partner"]] + pr["cross"]
-    w0 = [e * EW for e in order]
+    w0 = [e * ND for e in order]
     mz = [sem["mz%d" % i] for i in range(N)]
     cnt = [0]
 
@@ -190,18 +197,20 @@ def rank_program(g, core, T, topo):
         return (T.z0, T.z1)[src][:, 16 - 16 * dst:144 - 16 * dst]
 
     def child_rows(eng, i):
-        for grp in range(2):
-            eng.dma_start(T.W[16 * grp:128:32, w0[i]:w0[i] + EW], T.cl[order[i]] if i else tile(side)).then_inc(sem.wd, 16)
+        for bit in range(2):
+            a = 64 * bit
+            src = T.cl[order[i], a:a + 64, :] if i else T.cf[a:a + 64, 128 * side:128 * side + 128]
+            for grp in range(2):
+                eng.dma_start(T.W[16 * grp + 4 * bit:128:32, w0[i]:w0[i] + ND], src).then_inc(sem.wd, 16)
 
-    clears = [[(VFILL[0], 512), (VFILL[0] + 512, 512), (VFILL[0] + 1024, EW - VFILL[0] - 1024)]]
-    clears += [[(a, min(1024, EW - a)) for a in range(VFILL[i], EW, 1024)] for i in range(1, N)]
+    clears = [[(VFILL[0], 512), (VFILL[0] + 512, ND - VFILL[0] - 512)]] + [[(VFILL[i], ND - VFILL[i])] for i in range(1, N)]
     cleared = [1 + len(c) for c in clears]
 
-    sy.dma_start(T.ct[:, 0:128], T.child[0:8:2, :]).then_inc(sem.lc, 16)
-    sy.dma_start(T.ct[:, OWNQ:OWNQ + 32], T.ver[:]).then_inc(sem.lc, 16)
+    sy.dma_start(T.ct[:, OWNQ:OWNQ + 32], T.ver[:]).then_inc(sem.lq, 16)
+    sy.dma_start(T.ct[0:64, 0:256], T.child[0:8:2, :]).then_inc(sem.lc, 16)
     sy.dma_start(T.S[:, own:own + cut], T.sums[:, 0:cut]).then_inc(sem.ls0, 16)
     sy.dma_start(T.S[:, own + cut:own + ND], T.sums[:, cut:ND]).then_inc(sem.ls1, 16)
-    for i, arrived in enumerate(((sem.vconv, 1), (sem.parr, h4), (sem.carr0, len(off)))):
+    for i, arrived in enumerate(((sem.vconv, 4), (sem.parr, len(off)), (sem.carr0, len(off)))):
         sy.wait_ge(*arrived)
         sy.wait_ge(mz[i], cleared[i])
         child_rows(sy, i)
@@ -209,86 +218,90 @@ def rank_program(g, core, T, topo):
     sy.dma_start(T.y[:, 0:Q // 2], T.yo[:, 0:Q // 2]).then_inc(sem.st0, 16)
     sy.wait_ge(sem.st0, 16)
 
-    g.wait_ge(sem.vhalf, 1)
-    for a, z in enumerate((T.z0, T.z1)):
-        g.affine_select(z[:], T.half[:], [[32, 5], [1000, 2], [1, 16]], A.is_equal, 0.0, 16 * a - 1000, -1).then_inc(sem.gz, 1)
-    g.wait_ge(sem.vconv, 1)
-    g.remote_dma_fused(
-        [xfer(topo, core, tile(par), pr["near"][par], T.hc[:], on[h4 * par:h4 * (par + 1)], sem.harr) for par in range(2)] +
-        [xfer(topo, core, tile(1 - side), pc, T.cl[r], off[:h4], sem.parr),
-         xfer(topo, core, T.cf[:, OWNQ - 64:OWNQ + 64], pc, T.cf[:, PARQ - 64:PARQ + 64], off[h4:], sem.qarr)], local_sem=sem.sent)
+    g.wait_ge(sem.vone, 1)
+
+    def diagonal(a, done):
+        g.affine_select((T.z0, T.z1)[a][:], T.one[:], [[32, 5], [1000, 2], [1, 16]], A.is_equal, 0.0, 16 * a - 1000, -1).then_inc(done, 1)
+
+    diagonal(side, sem.gz)
+    g.wait_ge(sem.lq, 32)
+    g.remote_dma_fused([xfer(topo, core, T.ct[:, OWNQ:OWNQ + 64], pc, T.ct[:, PARQ:PARQ + 64], off, sem.qarr)], local_sem=sem.sent)
+    g.wait_ge(sem.vconv, 4)
+    g.remote_dma_fused([xfer(topo, core, tile(par), pr["near"][par], T.hc[:], (off, on)[par], sem.harr) for par in range(2)],
+                       local_sem=sem.sent)
+    g.remote_dma_fused([xfer(topo, core, tile(1 - side), pc, T.cl[r], off, sem.parr)], local_sem=sem.sent)
     he = hand_out_engines(P, topo, r)
 
     def hand_out(loaded, pieces):
         g.wait_ge(loaded, 16)
-        g.remote_dma_fused([xfer(topo, core, window(T, r, p), pr["carriers"][p], slot(T, p, 0), he[p], sem.sarr) for p in pieces],
+        g.remote_dma_fused([xfer(topo, core, window(T, r, p), pr["carriers"][p], slot(T, p), he[p], sem.sarr) for p in pieces],
                            local_sem=sem.sent)
 
-    def start_anew(first):
-        g.iota(T.dc[:, first:ODD + 512:4], [[0, (ODD + 512) // 4]], -H, 0, allow_small_or_imprecise_dtypes=True).then_inc(sem.gk, 1)
+    hand_out(sem.ls0, range(FIRST))
+    hand_out(sem.ls1, range(FIRST, 7))
+    diagonal(1 - side, sem.gi)
+    g.affine_select(T.idm[:], T.one[:, 0:128], [[-1, 128]], A.is_equal, 0.0, 0, 1).then_inc(sem.gi, 1)
+    arrivals = sum(len(off) if q == pr["partner"] or (q, p) in pr["via"] else h4 for q in order[1:] for p in range(7))
 
-    start_anew(0)
-    hand_out(sem.ls0, range(4))
-    hand_out(sem.ls1, range(4, 7))
-    start_anew(3)
-    g.wait_ge(sem.vone, 1)
-    g.affine_select(T.idm[:], T.one[:], [[-1, 128]], A.is_equal, 0.0, 0, 1).then_inc(sem.gi, 1)
-    arrivals = sum(len(off) if q == pr["partner"] or relayed(P, q, p, r) else h4 for q in order[1:] for p in range(7))
-
-    v.memset(T.half[:], 0.5).then_inc(sem.vhalf, 1)
+    v.memset(T.one[:], 1.0).then_inc(sem.vone, 1)
     v.memset(T.W[:, w0[3]:w0[3] + 512], 0.0).then_inc(sem.vw1, 1)
     v.memset(T.W[:, w0[3] + 512:w0[3] + 1536], 0.0).then_inc(sem.vw2, 1)
-    v.wait_ge(sem.lc, 64)
-    v.tensor_scalar(T.cf[:, 0:320], T.ct[:], 2.0, None, A.mult).then_inc(sem.vconv, 1)
-    v.memset(T.one[:], 1.0).then_inc(sem.vone, 1)
+    v.wait_ge(sem.lc, 32)
+    for par in range(2):
+        for bit in range(2):
+            v.tensor_copy(T.cf[64 * bit:64 * bit + 64, 128 * par:128 * par + 128],
+                          T.ct[64 * par:64 * par + 64, bit:256:2]).then_inc(sem.vconv, 1)
+    v.wait_ge(sem.lq, 32)
+    v.tensor_copy(T.cf[:, OWNQ:OWNQ + 64], T.ct[:, OWNQ:OWNQ + 64]).then_inc(sem.vq, 1)
     for i in range(N):
         a = 1536 if i == 3 else 0
         v.memset(T.W[:, w0[i] + a:w0[i] + VFILL[i]], 0.0).then_inc(mz[i], 1)
+    vop(v.memset(T.S[:, 0:SPAD], 0.0))
+    vop(v.memset(T.dc[:, 0:ODD + 512:4], -1.0 * H2))
+    v.wait_ge(sem.qarr, len(off))
+    v.tensor_copy(T.cf[:, PARQ:PARQ + 64], T.ct[:, PARQ:PARQ + 64]).then_inc(sem.vqp, 1)
     v.wait_ge(sem.pq, 1)
     vop(v.tensor_copy(T.dd[:, 0:64:2], T.px[:, 32:64]))
-    vop(v.tensor_scalar(T.dd[:, 1:64:2], T.py[:, 0:32], 2.0, None, A.mult))
-    vop(v.tensor_scalar(T.t0[:], T.px[:, 0:32], 2.0, float(2 * SPAD), A.mult, A.add))
-    vop(v.memset(T.S[:, 0:SPAD], 0.0))
+    vop(v.tensor_copy(T.dd[:, 1:64:2], T.py[:, 0:32]))
+    v.tensor_copy(T.ow[:, 0:32], T.px[:, 0:32]).then_inc(sem.vfirst, 1)
+    vop(v.tensor_scalar(T.t0[:], T.px[:, 0:32], float(SPAD), None, A.add))
     vwait()
-    for j in range(5):
-        vop(v.tensor_scalar(T.bb[:, 64 * j:64 * j + 64], T.dd[:], 9 - 2 * j, 1, A.arith_shift_right, A.bitwise_and))
+    for t in range(STEPS):
+        a = 64 * (t // 2)
+        vop(v.tensor_scalar((T.be, T.bo)[t % 2][:, a:a + 64], T.dd[:], 9 - t, 1, A.arith_shift_right, A.bitwise_and))
     vwait()
-    vop(v.tensor_tensor(T.i0[:], T.t0[:], T.bb[:, 0:64:2], A.add))
-    mask = (H + 2.0 * SPAD - 1, -1.0 * H, A.mult, A.add)
-    vop(v.tensor_copy(T.dc[:, 1:ODD:4], T.bb[:, 1:320:2]))
-    vop(v.tensor_scalar(T.dc[:, 2:ODD:4], T.bb[:, 1:320:2], *mask))
+    for a, b, this, following in ((0, ODD, T.be[:, 1:320:2], T.bo[:, 1:320:2]), (ODD, ODD + 512, T.bo[:, 0:256:2], T.be[:, 64:320:2])):
+        vop(v.tensor_scalar(T.dc[:, a + 1:b:4], this, -2.0 * H, 1.0 * H, A.mult, A.add))
+        vop(v.tensor_scalar(T.dc[:, a + 2:b:4], this, 1.0 * H, -1.0 * H, A.mult, A.add))
+        vop(v.tensor_scalar(T.dc[:, a + 3:b:4], following, 1.0 * (H2 + SPAD), -1.0 * H2, A.mult, A.add))
+    vop(v.tensor_tensor(T.son[:, 3:128:4], T.t0[:], T.be[:, 0:64:2], A.mult))
     vwait()
-    v.tensor_scalar(T.ow[:, 0:32], T.i0[:], -2.0 * SPAD, None, A.add).then_inc(sem.vfirst, 1)
-    vop(v.tensor_copy(T.dc[:, ODD + 1:ODD + 512:4], T.bb[:, 64:320:2]))
-    vop(v.tensor_scalar(T.dc[:, ODD + 2:ODD + 512:4], T.bb[:, 64:320:2], *mask))
-    vop(v.tensor_tensor(T.son[:, 2:128:4], T.t0[:], T.bb[:, 0:64:2], A.mult))
-    vwait()
-    v.wait_ge(sem.gk, 2)
 
-    s.dma_start(T.ct[:, 128:256], T.child[1:8:2, :]).then_inc(sem.lc, 16)
-    s.dma_start(T.ct[:, OWNQ + 32:OWNQ + 64], T.day[:]).then_inc(sem.lc, 16)
+    s.dma_start(T.ct[:, OWNQ + 32:OWNQ + 64], T.day[:]).then_inc(sem.lq, 16)
+    s.dma_start(T.ct[64:128, 0:256], T.child[1:8:2, :]).then_inc(sem.lc, 16)
     s.wait_ge(sem.vw1, 1)
     for i in range(N):
         for a, n in clears[i]:
-            if (i, a) == (0, VFILL[0] + 1024):
+            if (i, a) == (0, VFILL[0] + 512):
                 s.wait_ge(sem.vw2, 1)
             s.activation(T.W[:, w0[i] + a:w0[i] + a + n], T.W[:, w0[3]:w0[3] + n], COPY).then_inc(mz[i], 1)
     for i in range(N):
         s.wait_ge(mz[i], cleared[i])
+
     s.wait_ge(sem.carr1, len(off))
     child_rows(s, 3)
-    s.wait_ge(sem.wd, 8 * 16)
+    s.wait_ge(sem.wd, 16 * 16)
 
     def odd_days(q0, par):
         for c0 in range(2):
             mm = pe.matmul(T.py[:, par:32:2], shift(side, c0), T.cf[:, q0 + 32 + c0:q0 + 64:2], c0 == 0, c0 == 1)
         return mm
 
-    pe.wait_ge(sem.gz, 2)
-    pe.wait_ge(sem.vconv, 1)
+    pe.wait_ge(sem.gz, 1)
+    pe.wait_ge(sem.vq, 1)
     odd_days(OWNQ, side)
     pe.matmul(T.px[:, 0:64], shift(side, side), T.cf[:, OWNQ:OWNQ + 64], True, False)
-    pe.wait_ge(sem.qarr, h4)
+    pe.wait_ge(sem.vqp, 1)
     pe.matmul(T.px[:, 0:64], shift(side, 1 - side), T.cf[:, PARQ:PARQ + 64], False, True)
     odd_days(PARQ, 1 - side).then_inc(sem.pq, 1)
 
@@ -298,10 +311,10 @@ def rank_program(g, core, T, topo):
         return a1 - a0, c1 - c0, x, a0 + c0, len(STREAMS) * (a1 + c1 - 1)
 
     def even_nodes(b):
-        return T.son[:, 128 * BATCHES[b][0] + 2:128 * BATCHES[b][1]:4]
+        return T.son[:, 128 * BATCHES[b][0] + 3:128 * BATCHES[b][1]:4]
 
     def odd_nodes(b, par):
-        return T.sos[:, 128 * BATCHES[b][2] + 2 + 4 * par:128 * BATCHES[b][3]:8]
+        return T.sos[:, 128 * BATCHES[b][2] + 3 + 4 * par:128 * BATCHES[b][3]:8]
 
     copies = 0
     for b in range(len(BATCHES)):
@@ -314,21 +327,19 @@ def rank_program(g, core, T, topo):
         g.wait_ge(sem.gt, copies)
         width = 32 * ne + 16 * no
         g.remote_dma_fused([xfer(topo, core, T.tx[:, x:x + width], pc, T.rx[:, x:x + width], off, sem["lr%d" % b])], local_sem=sem.sent)
-    g.wait_ge(sem.sent, (1 + len(BATCHES)) * len(off) + len(on) + sum(len(x) for x in he))
+    g.wait_ge(sem.sent, (3 + len(BATCHES)) * len(off) + len(on) + sum(len(x) for x in he))
 
-    def turn_lists(b):
+    def turn_lists(b, mine):
         ne, no, x, _, scans = batch(b)
-        pu = T["pu%d" % b]
-        pe.wait_ge(sem.vs, scans)
-        pe.wait_ge(sem["lr%d" % b], len(off))
+        pu, to = T["pu%d" % b], side if mine else 1 - side
+        pe.wait_ge(*((sem.vs, scans) if mine else (sem["lr%d" % b], len(off))))
         if ne:
-            pe.matmul(pu[:, 0:32 * ne], shift(side, side), even_nodes(b), True, False)
-            pe.matmul(pu[:, 0:32 * ne], shift(side, 1 - side), T.rx[:, x:x + 32 * ne], False, True)
+            pe.matmul(pu[:, 0:32 * ne], shift(side, to), even_nodes(b) if mine else T.rx[:, x:x + 32 * ne], mine, False)
+        odd = odd_nodes(b, side) if mine else T.rx[:, x + 32 * ne:x + 32 * ne + 16 * no]
         for c0 in range(2):
-            out = pu[:, 32 * ne + c0:32 * (ne + no):2]
-            pe.matmul(out, shift(c0, side), odd_nodes(b, side), True, False)
-            mm = pe.matmul(out, shift(c0, 1 - side), T.rx[:, x + 32 * ne:x + 32 * ne + 16 * no], False, True)
-        mm.then_inc(sem["pl%d" % b], 1)
+            mm = pe.matmul(pu[:, 32 * ne + c0:32 * (ne + no):2], shift(c0, to), odd, mine and not ne and not c0, c0 == 1 and not mine)
+        if not mine:
+            mm.then_inc(sem["pl%d" % b], 1)
 
     def make_offsets(b):
         ne, no, _, j, _ = batch(b)
@@ -357,7 +368,7 @@ def rank_program(g, core, T, topo):
             if kp < STEPS - 2:
                 res, a, b = scanned(kp, hp)
                 o = 32 * (kp + 1)
-                v.tensor_copy(T.ow[:, o + STREAMS[hp][0]:o + STREAMS[hp][1]], res[:, a + 1:b:4]).then_inc(sem["so%d" % hp], 1)
+                v.tensor_copy(T.ow[:, o + STREAMS[hp][0]:o + STREAMS[hp][1]], res[:, a + 2:b:4]).then_inc(sem["so%d" % hp], 1)
         if (k, h) == (STEPS - 2, 1):
             make_offsets(0)
         v.wait_ge(sem.vt, i + 1)
@@ -371,41 +382,45 @@ def rank_program(g, core, T, topo):
         eng.wait_ge(sem.ls1, 16)
         eng.wait_ge(sem.sarr, arrivals)
 
-    def nodes(j, h=0, n=2):
-        return T.S[:, 0:SW].indirect(T.osm[:, 32 * j + 16 * h:32 * j + 16 * (h + n)])
+    def part(j, h, eng):
+        return ((0, 128) if eng is v else (128, 256)) if (j, h) == SHARED else (0, 256)
 
-    turn_lists(0)
-    pe.wait_ge(sem.gi, 1)
+    def nodes(j, h, eng):
+        a, b = part(j, h, eng)
+        return T.S[:, 0:SW].indirect(T.osm[:, 32 * j + 16 * h + a // 16:32 * j + 16 * h + b // 16])
+
+    pe.wait_ge(sem.gi, 2)
+    for b, mine in ((0, True), (0, False), (1, True), (2, True), (3, True), (1, False)):
+        turn_lists(b, mine)
     pa, va, pacc = (T.pa0, T.pa1), (sem.va0, sem.va1), (sem.pacc0, sem.pacc1)
-    for i, (u, j, h, n) in enumerate(((0, 0, 0, 1), (0, 0, 1, 1), (1, 1, 0, 1), (1, 1, 1, 1), (2, 2, 0, 2), (3, 6, 0, 2), (4, 7, 0, 2))):
-        sq, a = sem["sq%d" % i], Q * u + 256 * h
-        if u == 3:
-            s.wait_ge(sem.vl1, 1)
-        s.activation(T.gs[:, a:a + 256 * n], nodes(j, h, n), COPY).then_inc(sq, 1)
-        if u:
-            if u in (2, 3):
-                turn_lists(u - 1)
-            pe.wait_ge(sq, 1)
-            for hh in range(h, h + n):
-                mm = pe.matmul(pa[hh][:, 0:256], T.idm[:], T.gs[:, Q * u + 256 * hh:Q * u + 256 * hh + 256], u == 1, u == 4)
-                if u == 4:
-                    mm.then_inc(pacc[hh], 1)
-    for u, j in enumerate((3, 4, 5, 8, 9)):
-        for h in range(2):
-            c0, c1 = 256 * h, 256 * h + 256
-            if (j, h) == (5, 1):
-                make_offsets(1)
-            if (j, h) == (8, 1):
-                make_offsets(2)
-            if (j, h) in ((8, 0), (9, 0)):
-                v.wait_ge(sem["vl%d" % (j - 7)], 1)
-            v.wait_ge(*((va[h], u) if u else (sem["sq%d" % h], 1)))
-            v.tensor_tensor(T.acc[:, c0:c1], nodes(j, h, 1), (T.acc if u else T.gs)[:, c0:c1], A.add).then_inc(va[h], 1)
-    for h, vy in enumerate((sem.vy0, sem.vy1)):
+    batch_of = {batch(b)[3] + i: b for b in range(len(BATCHES)) for i in range(batch(b)[0] + batch(b)[1])}
+    for i, (j, h) in enumerate(ON_SCALAR):
+        a, b = part(j, h, s)
+        s.wait_ge(sem["vl%d" % batch_of[j]], 1)
+        s.activation(T.gs[:, 256 * i + a:256 * i + b], nodes(j, h, s), COPY).then_inc(sem["sq%d" % i], 1)
+    for n, (j, h) in enumerate(ADDED):
+        if (j, h) in TURN_AT:
+            turn_lists(TURN_AT[j, h], False)
+        i, last = ON_SCALAR.index((j, h)), h not in [u[1] for u in ADDED[n + 1:]]
+        pe.wait_ge(sem["sq%d" % i], 1)
+        a, b = part(j, h, s)
+        mm = pe.matmul(pa[h][:, a:b], T.idm[:], T.gs[:, 256 * i + a:256 * i + b], h not in [u[1] for u in ADDED[:n]], last)
+        if last:
+            mm.then_inc(pacc[h], 1)
+    done = [0, 0]
+    for j, h in ON_VECTOR:
+        c0, c1 = (256 * h + a for a in part(j, h, v))
+        if (j, h) in OFFSETS_AT:
+            make_offsets(OFFSETS_AT[j, h])
+        v.wait_ge(sem["vl%d" % batch_of[j]], 1)
+        v.wait_ge(*((va[h], done[h]) if done[h] else (sem["sq%d" % h], 1)))
+        v.tensor_tensor(T.acc[:, c0:c1], nodes(j, h, v), (T.acc if done[h] else T.gs)[:, c0:c1], A.add).then_inc(va[h], 1)
+        done[h] += 1
+    for h in range(2):
         c0, c1 = 256 * h, 256 * h + 256
-        v.wait_ge(va[h], 5)
+        v.wait_ge(va[h], done[h])
         v.wait_ge(pacc[h], 1)
-        v.tensor_tensor(T.yo[:, c0:c1], T.acc[:, c0:c1], pa[h][:, 0:256], A.add).then_inc(vy, 1)
+        v.tensor_tensor(T.yo[:, c0:c1], T.acc[:, c0:c1], pa[h][:, 0:256], A.add).then_inc(sem["vy%d" % h], 1)
     s.wait_ge(sem.vy1, 1)
     s.dma_start(T.y[:, Q // 2:Q], T.yo[:, Q // 2:Q]).then_inc(sem.st1, 16)
     s.wait_ge(sem.st1, 16)

from concourse.bass import DstId, RemoteDMATransfer
from concourse.mybir import AluOpType, ActivationFunctionType

N, ND, STEPS, Q = 4, 2048, 10, 512
WORLD = 256
FIRST = 4
WIDTH = (332, 240)
SPAD = 8
SW, WW = SPAD + N * ND, N * ND
H, H2 = 8192, 32768
VFILL = (768, 768, 768, 1792)
STREAMS = ((0, 12), (12, 22), (22, 32))
ODD = 640
OWNQ, PARQ = 256, 320
BATCHES = ((0, 2, 0, 2), (2, 4, 2, 3), (4, 5, 3, 4), (5, 5, 4, 5))
SHARED = (8, 1)
ON_SCALAR = [(j, h) for j in (0, 1, 4, 6, 8) for h in range(2)]
ON_VECTOR = [(j, h) for j in (2, 3, 5) for h in range(2)] + [(7, 1), (7, 0), (8, 1), (9, 0), (9, 1)]
ADDED = ON_SCALAR[2:7] + [(8, 0), (8, 1), (6, 1)]
TURN_AT = {(4, 1): 2, (6, 0): 3}
OFFSETS_AT = {(3, 0): 1, (7, 1): 2, (8, 1): 3}

SCRATCH = {
    "S": ("sbuf", [128, SW], "float32"),
    "W": ("sbuf", [128, WW], "float32"),
    "ct": ("sbuf", [128, 384], "int32"),
    "cf": ("sbuf", [128, 384], "float32"),
    "cl": ("dram", [N, 128, 128], "float32"),
    "hc": ("dram", [128, 128], "float32"),
    "h0": ("dram", [3, 128, WIDTH[0]], "float32"),
    "h1": ("dram", [3, 128, WIDTH[1]], "float32"),
    "dd": ("sbuf", [128, 64], "int32"),
    "be": ("sbuf", [128, 320], "int32"),
    "bo": ("sbuf", [128, 320], "int32"),
    "t0": ("sbuf", [128, 32], "float32"),
    "one": ("sbuf", [128, 160], "float32"),
    "z0": ("sbuf", [128, 160], "float32"),
    "z1": ("sbuf", [128, 160], "float32"),
    "idm": ("sbuf", [128, 128], "float32"),
    "dc": ("sbuf", [128, ODD + 512], "float32"),
    "son": ("sbuf", [128, 640], "float32"),
    "sos": ("sbuf", [128, 640], "float32"),
    "tx": ("sbuf", [128, 240], "float32"),
    "rx": ("sbuf", [128, 240], "float32"),
    "ow": ("sbuf", [128, 32 * 9], "uint16"),
    "osm": ("sbuf", [128, 320], "uint16"),
    "gw": ("sbuf", [128, Q], "float32"),
    "tw": ("sbuf", [128, Q], "float32"),
    "gs": ("sbuf", [128, 5 * Q], "float32"),
    "acc": ("sbuf", [128, Q], "float32"),
    "yo": ("sbuf", [128, Q], "float32"),
    "px": ("psum", [128, 512], "float32"),
    "py": ("psum", [128, 512], "float32"),
    "pu0": ("psum", [128, 512], "float32"),
    "pu1": ("psum", [128, 512], "float32"),
    "pu2": ("psum", [128, 512], "float32"),
    "pu3": ("psum", [128, 512], "float32"),
    "pa0": ("psum", [128, 512], "float32"),
    "pa1": ("psum", [128, 512], "float32"),
}
SEMAPHORES = ["lc", "lq", "vq", "vqp", "ls0", "ls1", "wd", "st0", "st1", "sent", "harr", "parr", "qarr", "carr0", "carr1", "sarr", "ra0", "ra1", "ra2",
              "lr0", "lr1", "lr2", "vv", "vw1", "vw2", "mz0", "mz1", "mz2", "mz3", "vconv", "vone", "vfirst", "vt", "vs",
              "vl0", "vl1", "vl2", "vy0", "vy1", "va0", "va1", "sg0", "sg1", "sg2", "so0", "so1", "so2",
              "sq0", "sq1", "sq2", "sq3", "sq4", "sq5", "sq6", "sq7", "sq8", "sq9", "gz", "gi", "gt", "pq", "pl0", "pl1", "pl2", "pl3", "lr3", "vl3", "pacc0", "pacc1"]

A = AluOpType
COPY = ActivationFunctionType.Copy


def mk(engines):
    return sum(1 << e for e in engines)


def plan(T, topo):
    P = []
    for r, c in enumerate(T.cores):
        partner = [q for q, d in enumerate(T.cores) if topo.same_plane(c, d)][0]
        cross = [q for q in range(N) if q not in (r, partner)]
        chip = [k for k in topo.cores_of(c) if k != c]
        ports = [k for k in chip if topo.may_write(k, T.cores[cross[0]])]
        here = [k for k in chip if topo.die(k) == topo.die(c)]
        near = [k for k in ports if k in here]
        far = [k for k in ports if k not in here]
        plain_near = [k for k in here if k not in ports]
        plain_far = [k for k in chip if k not in ports and k not in here]
        relays = [k for k in range(WORLD) if topo.mates(k, c) and topo.may_write(k, c)]
        carriers = [far[0], near[0], plain_far[0], plain_near[0], far[1], near[1], plain_far[1]]
        P.append(dict(core=c, partner=partner, side=int(r > partner), cross=cross, ports=ports, near=near, relays=relays,
                      carriers=carriers))
    for q, pq in enumerate(P):
        pq["via"] = {}
        for die in sorted(set(topo.die(k) for k in pq["relays"])):
            mine = [k for k in pq["relays"] if topo.die(k) == die]
            items = [(p, s) for s in range(N) if s != q for p, k in enumerate(P[s]["carriers"])
                     if topo.die(k) == die and relayed(P, s, p, q)]
            for i, (p, s) in enumerate(sorted(items)):
                pq["via"][s, p] = (mine[i % len(mine)], i // len(mine))
    return P


def relayed(P, r, p, q):
    k = P[r]["carriers"][p]
    return q != P[r]["partner"] and (k == P[r]["near"][1] or k not in P[r]["ports"])


def wave(p):
    return int(p >= FIRST)


def window(T, e, p):
    a = SPAD + e * ND + min(p, FIRST) * WIDTH[0] + max(p - FIRST, 0) * WIDTH[1]
    return T.S[:, a:a + WIDTH[wave(p)]]


def slot(T, p, i=0):
    return (T.h0, T.h1)[wave(p)][i]


def did(topo, dst, src):
    rid, pid = topo.addr(dst, src)
    return DstId(rid=rid, pnc=pid)


def xfer(topo, me, src, dst, ap, engines, sem):
    return RemoteDMATransfer(dst_ids=[did(topo, dst, me)], dma_engine_mask=mk(engines), remote_sem=sem, srcs=[src], dsts=[ap])


def hand_out_engines(P, topo, r):
    every = topo.engines(P[r]["core"], P[r]["near"][0])
    return [every[t::4] for t in range(4)] + [every[0::4], every[1::2], every[2::4]]


def helper_program(g, core, T, topo, P):
    sem = T.sem
    for r, pr in enumerate(P):
        if core in pr["carriers"]:
            p = pr["carriers"].index(core)
            eng = topo.engines(core, P[pr["partner"]]["core"])
            n, hf = len(eng), len(eng) // 2
            sent = 2 * n
            if core in pr["near"]:
                q = [q for q in pr["cross"] if P[q]["side"] == pr["near"].index(core)][0]
                g.wait_ge(sem.harr, n)
                g.remote_dma_fused([xfer(topo, core, T.hc[:], P[q]["core"], T.cl[r], eng, sem["carr%d" % P[q]["cross"].index(r)])],
                                   local_sem=sem.sent)
                sent += n
            g.wait_ge(sem.sarr, len(hand_out_engines(P, topo, r)[p]))
            alone, both = ([(eng, pr["partner"])], list(zip((eng[:hf], eng[hf:]), pr["cross"])))
            for call in ((both, alone) if relayed(P, r, p, pr["cross"][0]) else (alone, both)):
                moves = []
                for e, q in call:
                    if relayed(P, r, p, q):
                        k, i = P[q]["via"][r, p]
                        moves.append(xfer(topo, core, slot(T, p), k, slot(T, p, i), e, sem["ra%d" % i]))
                    else:
                        moves.append(xfer(topo, core, slot(T, p), P[q]["core"], window(T, r, p), e, sem.sarr))
                g.remote_dma_fused(moves, local_sem=sem.sent)
            g.wait_ge(sem.sent, sent)
        if core in pr["relays"]:
            eng = topo.engines(core, pr["core"])
            mine = sorted((i, s, p) for (s, p), (k, i) in pr["via"].items() if k == core)
            for i, s, p in mine:
                g.wait_ge(sem["ra%d" % i], len(eng) if s == pr["partner"] else len(eng) // 2)
                g.remote_dma_fused([xfer(topo, core, slot(T, p, i), pr["core"], window(T, s, p), eng, sem.sarr)], local_sem=sem.sent)
            g.wait_ge(sem.sent, len(eng) * len(mine))


def rank_program(g, core, T, topo):
    P = plan(T, topo)
    r = T.rank_of(core)
    if r is None:
        helper_program(g, core, T, topo, P)
        return
    sem, pr = T.sem, P[r]
    v, s, sy, pe = g.vector, g.scalar, g.sync, g.tensor
    pc, side = P[pr["partner"]]["core"], pr["side"]
    off = topo.engines(core, pc)
    on = [e for e in topo.engines(core, pr["near"][0]) if e not in off]
    h4 = len(off) // 2
    own, cut = SPAD + r * ND, FIRST * WIDTH[0]
    order = [r, pr["partner"]] + pr["cross"]
    w0 = [e * ND for e in order]
    mz = [sem["mz%d" % i] for i in range(N)]
    cnt = [0]

    def vop(ins):
        ins.then_inc(sem.vv, 1)
        cnt[0] += 1

    def vwait():
        v.wait_ge(sem.vv, cnt[0])

    def tile(par):
        return T.cf[:, 128 * par:128 * par + 128]

    def shift(src, dst):
        return (T.z0, T.z1)[src][:, 16 - 16 * dst:144 - 16 * dst]

    def child_rows(eng, i):
        for bit in range(2):
            a = 64 * bit
            src = T.cl[order[i], a:a + 64, :] if i else T.cf[a:a + 64, 128 * side:128 * side + 128]
            for grp in range(2):
                eng.dma_start(T.W[16 * grp + 4 * bit:128:32, w0[i]:w0[i] + ND], src).then_inc(sem.wd, 16)

    clears = [[(VFILL[0], 512), (VFILL[0] + 512, ND - VFILL[0] - 512)]] + [[(VFILL[i], ND - VFILL[i])] for i in range(1, N)]
    cleared = [1 + len(c) for c in clears]

    sy.dma_start(T.ct[:, OWNQ:OWNQ + 32], T.ver[:]).then_inc(sem.lq, 16)
    sy.dma_start(T.ct[0:64, 0:256], T.child[0:8:2, :]).then_inc(sem.lc, 16)
    sy.dma_start(T.S[:, own:own + cut], T.sums[:, 0:cut]).then_inc(sem.ls0, 16)
    sy.dma_start(T.S[:, own + cut:own + ND], T.sums[:, cut:ND]).then_inc(sem.ls1, 16)
    for i, arrived in enumerate(((sem.vconv, 4), (sem.parr, len(off)), (sem.carr0, len(off)))):
        sy.wait_ge(*arrived)
        sy.wait_ge(mz[i], cleared[i])
        child_rows(sy, i)
    sy.wait_ge(sem.vy0, 1)
    sy.dma_start(T.y[:, 0:Q // 2], T.yo[:, 0:Q // 2]).then_inc(sem.st0, 16)
    sy.wait_ge(sem.st0, 16)

    g.wait_ge(sem.vone, 1)

    def diagonal(a, done):
        g.affine_select((T.z0, T.z1)[a][:], T.one[:], [[32, 5], [1000, 2], [1, 16]], A.is_equal, 0.0, 16 * a - 1000, -1).then_inc(done, 1)

    diagonal(side, sem.gz)
    g.wait_ge(sem.lq, 32)
    g.remote_dma_fused([xfer(topo, core, T.ct[:, OWNQ:OWNQ + 64], pc, T.ct[:, PARQ:PARQ + 64], off, sem.qarr)], local_sem=sem.sent)
    g.wait_ge(sem.vconv, 4)
    g.remote_dma_fused([xfer(topo, core, tile(par), pr["near"][par], T.hc[:], (off, on)[par], sem.harr) for par in range(2)],
                       local_sem=sem.sent)
    g.remote_dma_fused([xfer(topo, core, tile(1 - side), pc, T.cl[r], off, sem.parr)], local_sem=sem.sent)
    he = hand_out_engines(P, topo, r)

    def hand_out(loaded, pieces):
        g.wait_ge(loaded, 16)
        g.remote_dma_fused([xfer(topo, core, window(T, r, p), pr["carriers"][p], slot(T, p), he[p], sem.sarr) for p in pieces],
                           local_sem=sem.sent)

    hand_out(sem.ls0, range(FIRST))
    hand_out(sem.ls1, range(FIRST, 7))
    diagonal(1 - side, sem.gi)
    g.affine_select(T.idm[:], T.one[:, 0:128], [[-1, 128]], A.is_equal, 0.0, 0, 1).then_inc(sem.gi, 1)
    arrivals = sum(len(off) if q == pr["partner"] or (q, p) in pr["via"] else h4 for q in order[1:] for p in range(7))

    v.memset(T.one[:], 1.0).then_inc(sem.vone, 1)
    v.memset(T.W[:, w0[3]:w0[3] + 512], 0.0).then_inc(sem.vw1, 1)
    v.memset(T.W[:, w0[3] + 512:w0[3] + 1536], 0.0).then_inc(sem.vw2, 1)
    v.wait_ge(sem.lc, 32)
    for par in range(2):
        for bit in range(2):
            v.tensor_copy(T.cf[64 * bit:64 * bit + 64, 128 * par:128 * par + 128],
                          T.ct[64 * par:64 * par + 64, bit:256:2]).then_inc(sem.vconv, 1)
    v.wait_ge(sem.lq, 32)
    v.tensor_copy(T.cf[:, OWNQ:OWNQ + 64], T.ct[:, OWNQ:OWNQ + 64]).then_inc(sem.vq, 1)
    for i in range(N):
        a = 1536 if i == 3 else 0
        v.memset(T.W[:, w0[i] + a:w0[i] + VFILL[i]], 0.0).then_inc(mz[i], 1)
    vop(v.memset(T.S[:, 0:SPAD], 0.0))
    vop(v.memset(T.dc[:, 0:ODD + 512:4], -1.0 * H2))
    v.wait_ge(sem.qarr, len(off))
    v.tensor_copy(T.cf[:, PARQ:PARQ + 64], T.ct[:, PARQ:PARQ + 64]).then_inc(sem.vqp, 1)
    v.wait_ge(sem.pq, 1)
    vop(v.tensor_copy(T.dd[:, 0:64:2], T.px[:, 32:64]))
    vop(v.tensor_copy(T.dd[:, 1:64:2], T.py[:, 0:32]))
    v.tensor_copy(T.ow[:, 0:32], T.px[:, 0:32]).then_inc(sem.vfirst, 1)
    vop(v.tensor_scalar(T.t0[:], T.px[:, 0:32], float(SPAD), None, A.add))
    vwait()
    for t in range(STEPS):
        a = 64 * (t // 2)
        vop(v.tensor_scalar((T.be, T.bo)[t % 2][:, a:a + 64], T.dd[:], 9 - t, 1, A.arith_shift_right, A.bitwise_and))
    vwait()
    for a, b, this, following in ((0, ODD, T.be[:, 1:320:2], T.bo[:, 1:320:2]), (ODD, ODD + 512, T.bo[:, 0:256:2], T.be[:, 64:320:2])):
        vop(v.tensor_scalar(T.dc[:, a + 1:b:4], this, -2.0 * H, 1.0 * H, A.mult, A.add))
        vop(v.tensor_scalar(T.dc[:, a + 2:b:4], this, 1.0 * H, -1.0 * H, A.mult, A.add))
        vop(v.tensor_scalar(T.dc[:, a + 3:b:4], following, 1.0 * (H2 + SPAD), -1.0 * H2, A.mult, A.add))
    vop(v.tensor_tensor(T.son[:, 3:128:4], T.t0[:], T.be[:, 0:64:2], A.mult))
    vwait()

    s.dma_start(T.ct[:, OWNQ + 32:OWNQ + 64], T.day[:]).then_inc(sem.lq, 16)
    s.dma_start(T.ct[64:128, 0:256], T.child[1:8:2, :]).then_inc(sem.lc, 16)
    s.wait_ge(sem.vw1, 1)
    for i in range(N):
        for a, n in clears[i]:
            if (i, a) == (0, VFILL[0] + 512):
                s.wait_ge(sem.vw2, 1)
            s.activation(T.W[:, w0[i] + a:w0[i] + a + n], T.W[:, w0[3]:w0[3] + n], COPY).then_inc(mz[i], 1)
    for i in range(N):
        s.wait_ge(mz[i], cleared[i])

    s.wait_ge(sem.carr1, len(off))
    child_rows(s, 3)
    s.wait_ge(sem.wd, 16 * 16)

    def odd_days(q0, par):
        for c0 in range(2):
            mm = pe.matmul(T.py[:, par:32:2], shift(side, c0), T.cf[:, q0 + 32 + c0:q0 + 64:2], c0 == 0, c0 == 1)
        return mm

    pe.wait_ge(sem.gz, 1)
    pe.wait_ge(sem.vq, 1)
    odd_days(OWNQ, side)
    pe.matmul(T.px[:, 0:64], shift(side, side), T.cf[:, OWNQ:OWNQ + 64], True, False)
    pe.wait_ge(sem.vqp, 1)
    pe.matmul(T.px[:, 0:64], shift(side, 1 - side), T.cf[:, PARQ:PARQ + 64], False, True)
    odd_days(PARQ, 1 - side).then_inc(sem.pq, 1)

    def batch(b):
        a0, a1, c0, c1 = BATCHES[b]
        x = sum(32 * (u[1] - u[0]) + 16 * (u[3] - u[2]) for u in BATCHES[:b])
        return a1 - a0, c1 - c0, x, a0 + c0, len(STREAMS) * (a1 + c1 - 1)

    def even_nodes(b):
        return T.son[:, 128 * BATCHES[b][0] + 3:128 * BATCHES[b][1]:4]

    def odd_nodes(b, par):
        return T.sos[:, 128 * BATCHES[b][2] + 3 + 4 * par:128 * BATCHES[b][3]:8]

    copies = 0
    for b in range(len(BATCHES)):
        ne, no, x, _, scans = batch(b)
        g.wait_ge(sem.vs, scans)
        for n, a, src in ((32 * ne, x, even_nodes), (16 * no, x + 32 * ne, lambda b: odd_nodes(b, 1 - side))):
            if n:
                g.affine_select(T.tx[:, a:a + n], src(b), [[0, n]], A.is_equal, 0.0, 0, 0).then_inc(sem.gt, 1)
                copies += 1
        g.wait_ge(sem.gt, copies)
        width = 32 * ne + 16 * no
        g.remote_dma_fused([xfer(topo, core, T.tx[:, x:x + width], pc, T.rx[:, x:x + width], off, sem["lr%d" % b])], local_sem=sem.sent)
    g.wait_ge(sem.sent, (3 + len(BATCHES)) * len(off) + len(on) + sum(len(x) for x in he))

    def turn_lists(b, mine):
        ne, no, x, _, scans = batch(b)
        pu, to = T["pu%d" % b], side if mine else 1 - side
        pe.wait_ge(*((sem.vs, scans) if mine else (sem["lr%d" % b], len(off))))
        if ne:
            pe.matmul(pu[:, 0:32 * ne], shift(side, to), even_nodes(b) if mine else T.rx[:, x:x + 32 * ne], mine, False)
        odd = odd_nodes(b, side) if mine else T.rx[:, x + 32 * ne:x + 32 * ne + 16 * no]
        for c0 in range(2):
            mm = pe.matmul(pu[:, 32 * ne + c0:32 * (ne + no):2], shift(c0, to), odd, mine and not ne and not c0, c0 == 1 and not mine)
        if not mine:
            mm.then_inc(sem["pl%d" % b], 1)

    def make_offsets(b):
        ne, no, _, j, _ = batch(b)
        v.wait_ge(sem["pl%d" % b], 1)
        v.tensor_copy(T.osm[:, 32 * j:32 * (j + ne + no)], T["pu%d" % b][:, 0:32 * (ne + no)]).then_inc(sem["vl%d" % b], 1)

    slots = [(k, h) for k in range(STEPS - 1) for h in range(len(STREAMS))]

    def scanned(k, h):
        c0, c1 = STREAMS[h]
        res, b = (T.son, 128 * (k // 2 + 1)) if k % 2 else (T.sos, 128 * (k // 2))
        return res, b + 4 * c0, b + 4 * c1

    s.wait_ge(sem.vfirst, 1)
    for i, (k, h) in enumerate(slots):
        c0, c1 = STREAMS[h]
        sg, so = sem["sg%d" % h], sem["so%d" % h]
        if k:
            s.wait_ge(so, k)
        s.activation(T.gw[:, 16 * c0:16 * c1], T.W[:, 0:WW].indirect(T.ow[:, 32 * k + c0:32 * k + c1]), COPY).then_inc(sg, 1)
        v.wait_ge(sg, k + 1)
        v.transpose(T.tw[:, 16 * c0:16 * c1], T.gw[:, 16 * c0:16 * c1]).then_inc(sem.vt, 1)
        if i:
            v.wait_ge(sem.vs, i)
            kp, hp = slots[i - 1]
            if kp < STEPS - 2:
                res, a, b = scanned(kp, hp)
                o = 32 * (kp + 1)
                v.tensor_copy(T.ow[:, o + STREAMS[hp][0]:o + STREAMS[hp][1]], res[:, a + 2:b:4]).then_inc(sem["so%d" % hp], 1)
        if (k, h) == (STEPS - 2, 1):
            make_offsets(0)
        v.wait_ge(sem.vt, i + 1)
        res, a, b = scanned(k, h)
        d = 128 * (k // 2) + (ODD if k % 2 else 0)
        v.tensor_tensor_scan(res[:, a:b], T.dc[:, d + 4 * c0:d + 4 * c1], T.tw[:, 16 * c0:16 * c1:4], 0.0, A.add, A.max).then_inc(sem.vs, 1)

    for eng in (s, v):
        eng.wait_ge(sem.vl0, 1)
        eng.wait_ge(sem.ls0, 16)
        eng.wait_ge(sem.ls1, 16)
        eng.wait_ge(sem.sarr, arrivals)

    def part(j, h, eng):
        return ((0, 128) if eng is v else (128, 256)) if (j, h) == SHARED else (0, 256)

    def nodes(j, h, eng):
        a, b = part(j, h, eng)
        return T.S[:, 0:SW].indirect(T.osm[:, 32 * j + 16 * h + a // 16:32 * j + 16 * h + b // 16])

    pe.wait_ge(sem.gi, 2)
    for b, mine in ((0, True), (0, False), (1, True), (2, True), (3, True), (1, False)):
        turn_lists(b, mine)
    pa, va, pacc = (T.pa0, T.pa1), (sem.va0, sem.va1), (sem.pacc0, sem.pacc1)
    batch_of = {batch(b)[3] + i: b for b in range(len(BATCHES)) for i in range(batch(b)[0] + batch(b)[1])}
    for i, (j, h) in enumerate(ON_SCALAR):
        a, b = part(j, h, s)
        s.wait_ge(sem["vl%d" % batch_of[j]], 1)
        s.activation(T.gs[:, 256 * i + a:256 * i + b], nodes(j, h, s), COPY).then_inc(sem["sq%d" % i], 1)
    for n, (j, h) in enumerate(ADDED):
        if (j, h) in TURN_AT:
            turn_lists(TURN_AT[j, h], False)
        i, last = ON_SCALAR.index((j, h)), h not in [u[1] for u in ADDED[n + 1:]]
        pe.wait_ge(sem["sq%d" % i], 1)
        a, b = part(j, h, s)
        mm = pe.matmul(pa[h][:, a:b], T.idm[:], T.gs[:, 256 * i + a:256 * i + b], h not in [u[1] for u in ADDED[:n]], last)
        if last:
            mm.then_inc(pacc[h], 1)
    done = [0, 0]
    for j, h in ON_VECTOR:
        c0, c1 = (256 * h + a for a in part(j, h, v))
        if (j, h) in OFFSETS_AT:
            make_offsets(OFFSETS_AT[j, h])
        v.wait_ge(sem["vl%d" % batch_of[j]], 1)
        v.wait_ge(*((va[h], done[h]) if done[h] else (sem["sq%d" % h], 1)))
        v.tensor_tensor(T.acc[:, c0:c1], nodes(j, h, v), (T.acc if done[h] else T.gs)[:, c0:c1], A.add).then_inc(va[h], 1)
        done[h] += 1
    for h in range(2):
        c0, c1 = 256 * h, 256 * h + 256
        v.wait_ge(va[h], done[h])
        v.wait_ge(pacc[h], 1)
        v.tensor_tensor(T.yo[:, c0:c1], T.acc[:, c0:c1], pa[h][:, 0:256], A.add).then_inc(sem["vy%d" % h], 1)
    s.wait_ge(sem.vy1, 1)
    s.dma_start(T.y[:, Q // 2:Q], T.yo[:, Q // 2:Q]).then_inc(sem.st1, 16)
    s.wait_ge(sem.st1, 16)
